import numpy as np
import ml_dtypes


def mxq(x, axis, fmt="e4m3"):
    dtype, down = {"e4m3": (ml_dtypes.float8_e4m3fn, 7), "e5m2": (ml_dtypes.float8_e5m2, 14)}[fmt]
    v = np.moveaxis(np.asarray(x, np.float32).astype(ml_dtypes.bfloat16).astype(np.float64), axis, -1)
    blocks = v.reshape(v.shape[:-1] + (-1, 32))
    amax = np.abs(blocks).max(-1, keepdims=True)
    byte = np.maximum(np.where(amax > 0, np.frexp(amax)[1] - 1 + 127, 0) - down, 1)
    scale = np.exp2(byte - 127.0)
    codes = (blocks / scale).astype(np.float32).astype(dtype).astype(np.float64)
    return np.moveaxis((codes * scale).reshape(v.shape), -1, axis)


WIDE = False


def mx_kscale(k):
    if not WIDE:
        return np.ones(k)
    levels = np.array([10, -10, 5, -5, 0])
    if k % 512:
        return np.exp2(np.random.permutation(np.resize(levels, k // 32))).repeat(32)
    a = np.empty((k // 512, 16))
    for p in range(k // 512):
        a[p, :8] = np.random.permutation(np.resize(levels, 8))
        for g in range(8):
            far = levels[np.abs(levels - a[p, g]) >= 10]
            a[p, g + 8] = far[np.random.randint(len(far))]
    return np.exp2(a.ravel()).repeat(32)


def f64(x):
    return np.asarray(x).astype(np.float64)


def striped(idx):
    return np.tile(np.asarray(idx).reshape(-1, 16).T, (8, 1)).astype(np.uint16)


def unstriped(offs):
    return offs[:16].T.reshape(-1).astype(np.int64)


def striped8(idx):
    return np.asarray(idx).reshape(8, -1, 16).transpose(0, 2, 1).reshape(128, -1).astype(np.uint16)


def unstriped8(offs):
    return offs.reshape(8, 16, -1).transpose(0, 2, 1).reshape(8, -1).astype(np.int64)


def pick8(x, idx, run):
    r = np.arange(len(x))
    return x[r[:, None], idx[r % (8 * run) // run]]


def bf(x):
    return np.asarray(x, np.float32).astype(ml_dtypes.bfloat16)


def planes(Y):
    r, m = Y.shape
    b = f64(bf(Y)).reshape(r // 32, 32, m)
    amax = np.abs(b).max(1)
    byte = np.clip(np.where(amax > 0, np.frexp(amax)[1] - 1 + 127 - 7, 1), 1, 254)
    codes = (b * np.exp2(127.0 - byte)[:, None, :]).reshape(r, m).astype(np.float32).astype(ml_dtypes.float8_e4m3fn).view(np.uint8)
    words = codes.reshape(r // 512, 128, 4, m).transpose(0, 1, 3, 2)
    return np.ascontiguousarray(words), np.ascontiguousarray(byte.astype(np.uint8).reshape(r // 512, 16, m))


D, T, I, C, F = 512, 2048, 512, 1024, 512


def setup_inputs():
    n = np.random.standard_normal
    idx = np.random.permutation(T)[:I]
    idx2 = np.stack([np.random.randint(0, C, I) for _ in range(8)])
    fd = mx_kscale(D)
    return {
        "vec": (n((D, T)) / fd[:, None]).astype(np.float32),
        "book": (n((D, C)) * 0.8 / fd[:, None]).astype(np.float32),
        "wo": (n((D, F)) * 1 / np.sqrt(D) * fd[:, None]).astype(np.float32),
        "bias": (0.3 * n((F, 1))).astype(np.float32),
        "offs": striped(idx),
        "offs2": striped8(idx2),
    }


def reference(vec, book, wo, bias, offs, offs2):
    idx = unstriped(offs)
    idx2 = unstriped8(offs2)
    x = f64(vec)[:, idx] - pick8(f64(book), idx2, 64)
    woq = mxq(f64(wo), 0, "e4m3")
    xq = mxq(x, 0, "e4m3")
    z = woq.T @ xq
    y = z + f64(bias)
    words, scales = planes(y)
    return y, words, scales

@@ -1,0 +1,156 @@
+from contextlib import ExitStack
+
+import concourse.mybir as mybir
+
+D, T, I, C, F = 512, 2048, 512, 1024, 512
+FLOPS = 2 * D * F * I
+
+F32 = mybir.dt.float32
+BF16 = mybir.dt.bfloat16
+I32 = mybir.dt.int32
+U32 = mybir.dt.uint32
+U16 = mybir.dt.uint16
+U8 = mybir.dt.uint8
+FP8X4 = mybir.dt.float8_e4m3fn_x4
+SUB = mybir.AluOpType.subtract
+IDENT = mybir.ActivationFunctionType.Identity
+
+P = 128
+PACK = 4
+CH = 128
+NCH = I // CH
+OC = CH // 16
+HALF = 256
+WO_SPLIT = (84, 64)
+
+
+def tile_attend_pqremainder_pl_kernel(tc, vec, book, wo, bias, offs, offs2, out_0, out_1, out_2):
+    nc = tc.nc
+    with ExitStack() as ctx:
+        sb = ctx.enter_context(tc.tile_pool(name="sb", bufs=1))
+        ps = ctx.enter_context(tc.psum_pool(name="ps", bufs=1))
+
+        offs_t = sb.tile([P, I // 16], U16, name="offs_t")
+        offs2_t = sb.tile([P, I // 16], U16, name="offs2_t")
+        bias_t = sb.tile([P, PACK], F32, name="bias_t")
+        book_t = [sb.tile([P, C], F32, name="book%d" % t) for t in range(PACK)]
+        vec_t = [sb.tile([P, T], F32, name="vec%d" % t) for t in range(PACK)]
+        wo_raw = sb.tile([P, PACK, F], F32, name="wo_raw")
+
+        book_v = book.rearrange("(p t) c -> p t c", t=PACK)
+        vec_v = vec.rearrange("(p t) c -> p t c", t=PACK)
+        nc.sync.dma_start(book_t[0][:], book_v[:, 0, :])
+        nc.sync.dma_start(offs2_t[:], offs2)
+        nc.sync.dma_start(offs_t[:], offs)
+        nc.sync.dma_start(bias_t[:], bias.rearrange("(p j) o -> p (j o)", j=PACK))
+        for t in range(1, PACK):
+            nc.sync.dma_start(book_t[t][:], book_v[:, t, :])
+        for t in range(PACK):
+            nc.sync.dma_start(vec_t[t][:], vec_v[:, t, :])
+        nc.sync.dma_start(wo_raw[:], wo.rearrange("(p t) f -> p t f", t=PACK))
+
+        picked = [sb.tile([P, I], F32, name="picked%d" % t) for t in range(PACK)]
+        for t in range(PACK):
+            nc.vector.tensor_copy(picked[t][:], book_t[t][:].indirect(offs2_t[:]))
+
+        x01 = sb.tile([P, 2, I], F32, name="x01")
+        x23 = [sb.tile([P, 2, CH], F32, name="x23_%d" % c) for c in range(NCH)]
+        xb = [sb.tile([P, CH, PACK], BF16, name="xb%d" % c, align_bytes=64) for c in range(NCH)]
+        x_codes = sb.tile([P, I], U32, name="x_codes", align_bytes=64)
+        x_scales = sb.tile([P, I], U8, name="x_scales", align_bytes=64)
+
+        for t in range(2):
+            nc.vector.tensor_tensor(x01[:, t, :], vec_t[t][:].indirect(offs_t[:]), picked[t][:], SUB)
+        for c in range(NCH):
+            cols = slice(c * CH, (c + 1) * CH)
+            nc.scalar.activation(xb[c][:, :, 0:2], x01[:, :, cols].rearrange("p t i -> p i t"), IDENT)
+        for t in range(2, PACK):
+            for c in range(NCH):
+                cols = slice(c * CH, (c + 1) * CH)
+                nc.vector.tensor_tensor(
+                    x23[c][:, t - 2, :],
+                    vec_t[t][:].indirect(offs_t[:, c * OC : (c + 1) * OC]),
+                    picked[t][:, cols],
+                    SUB,
+                )
+        for c in range(NCH):
+            cols = slice(c * CH, (c + 1) * CH)
+            nc.scalar.activation(xb[c][:, :, 2:4], x23[c][:].rearrange("p t i -> p i t"), IDENT)
+            nc.vector.quantize_mx(
+                out=x_codes[:, cols].bitcast(FP8X4),
+                scales=x_scales[:, cols],
+                in_=xb[c][:].rearrange("p i t -> p (i t)"),
+            )
+
+        w_codes = sb.tile([P, F], U32, name="w_codes", align_bytes=64)
+        w_scales = sb.tile([P, F], U8, name="w_scales", align_bytes=64)
+        wo_v = wo_raw[:].rearrange("p t (m j) -> p m j t", j=PACK)
+        for u in range(2):
+            wb = sb.tile([P, 2, P, PACK], BF16, name="wb%d" % u, align_bytes=64)
+            wb_v = wb[:].rearrange("p j m t -> p m j t")
+            s = WO_SPLIT[u]
+            nc.vector.tensor_copy(wb_v[:, 0:s, :, :], wo_v[:, 0:s, 2 * u : 2 * u + 2, :])
+            nc.scalar.activation(wb_v[:, s:P, :, :], wo_v[:, s:P, 2 * u : 2 * u + 2, :], IDENT)
+            for e in range(2):
+                j = 2 * u + e
+                cols = slice(j * P, (j + 1) * P)
+                nc.vector.quantize_mx(
+                    out=w_codes[:, cols].bitcast(FP8X4),
+                    scales=w_scales[:, cols],
+                    in_=wb[:, e, :, :].rearrange("p m t -> p (m t)"),
+                )
+
+        y_codes = sb.tile([P, I], U32, name="y_codes", align_bytes=64)
+        y_scales = sb.tile([P, I], U8, name="y_scales", align_bytes=64)
+        out0_v = out_0.rearrange("(p j) i -> p j i", j=PACK)
+        words_v = out_1[0].rearrange("l c r -> l (c r)").bitcast(I32)
+        scales_v = out_2[0].bitcast(I32)
+
+        def quantize_y(yb, cols):
+            nc.vector.quantize_mx(
+                out=y_codes[:, cols].bitcast(FP8X4),
+                scales=y_scales[:, cols],
+                in_=yb[:].rearrange("p i j -> p (i j)"),
+            )
+
+        for h in range(2):
+            hc = slice(h * HALF, (h + 1) * HALF)
+            y = sb.tile([P, PACK, HALF], F32, name="y%d" % h)
+            for j in range(PACK):
+                acc = ps.tile([P, HALF], F32, name="acc%d_%d" % (h, j))
+                wc = slice(j * P, (j + 1) * P)
+                nc.tensor.matmul_mx(
+                    out=acc[:],
+                    lhsT=w_codes[:, wc].bitcast(FP8X4),
+                    lhsT_scale=w_scales[:, wc],
+                    rhs=x_codes[:, hc].bitcast(FP8X4),
+                    rhs_scale=x_scales[:, hc],
+                    start=True,
+                    stop=True,
+                )
+                if h == 0 and j % 2 == 1:
+                    nc.vector.tensor_scalar_add(y[:, j, :], acc[:], bias_t[:, j : j + 1])
+                else:
+                    nc.scalar.activation(y[:, j, :], acc[:], IDENT, bias=bias_t[:, j : j + 1])
+            nc.sync.dma_start(out0_v[:, :, hc], y[:])
+            if h == 0:
+                yb = sb.tile([P, HALF, PACK], BF16, name="yb0", align_bytes=64)
+                nc.vector.tensor_copy(
+                    yb[:].rearrange("p (c i) j -> p c j i", i=4),
+                    y[:].rearrange("p j (c i) -> p c j i", i=4),
+                )
+                quantize_y(yb, hc)
+            else:
+                for e in range(2):
+                    yb = sb.tile([P, CH, PACK], BF16, name="yb1_%d" % e, align_bytes=64)
+                    dst = yb[:].rearrange("p (c i) j -> p c j i", i=4)
+                    src = y[:, :, e * CH : (e + 1) * CH].rearrange("p j (c i) -> p c j i", i=4)
+                    if e == 0:
+                        nc.vector.tensor_copy(dst, src)
+                    else:
+                        nc.scalar.activation(dst, src, IDENT)
+                    quantize_y(yb, slice(HALF + e * CH, HALF + (e + 1) * CH))
+            nc.sync.dma_start(words_v[:, hc], y_codes[:, hc].bitcast(I32))
+        for q in range(4):
+            queue = nc.sync if q < 2 else nc.scalar
+            queue.dma_start(scales_v[4 * q : 4 * q + 4, :], y_scales[32 * q : 32 * q + 4, :].bitcast(I32))

@@ -13,6 +13,7 @@ U16 = mybir.dt.uint16
 U8 = mybir.dt.uint8
 FP8X4 = mybir.dt.float8_e4m3fn_x4
 SUB = mybir.AluOpType.subtract
+ADD = mybir.AluOpType.add
 IDENT = mybir.ActivationFunctionType.Identity
 
 P = 128
@@ -21,7 +22,7 @@ CH = 128
 NCH = I // CH
 OC = CH // 16
 HALF = 256
-WO_SPLIT = (84, 64)
+WO_SPLIT = (128, 64)
 
 
 def tile_attend_pqremainder_pl_kernel(tc, vec, book, wo, bias, offs, offs2, out_0, out_1, out_2):
@@ -42,115 +43,115 @@ def tile_attend_pqremainder_pl_kernel(tc, vec, book, wo, bias, offs, offs2, out_
         nc.sync.dma_start(book_t[0][:], book_v[:, 0, :])
         nc.sync.dma_start(offs2_t[:], offs2)
         nc.sync.dma_start(offs_t[:], offs)
-        nc.sync.dma_start(bias_t[:], bias.rearrange("(p j) o -> p (j o)", j=PACK))
         for t in range(1, PACK):
             nc.sync.dma_start(book_t[t][:], book_v[:, t, :])
         for t in range(PACK):
             nc.sync.dma_start(vec_t[t][:], vec_v[:, t, :])
         nc.sync.dma_start(wo_raw[:], wo.rearrange("(p t) f -> p t f", t=PACK))
+        nc.sync.dma_start(bias_t[:], bias.rearrange("(p j) o -> p (j o)", j=PACK))
 
         picked = [sb.tile([P, I], F32, name="picked%d" % t) for t in range(PACK)]
         for t in range(PACK):
             nc.vector.tensor_copy(picked[t][:], book_t[t][:].indirect(offs2_t[:]))
 
         x01 = sb.tile([P, 2, I], F32, name="x01")
-        x23 = [sb.tile([P, 2, CH], F32, name="x23_%d" % c) for c in range(NCH)]
-        xb = [sb.tile([P, CH, PACK], BF16, name="xb%d" % c, align_bytes=64) for c in range(NCH)]
-        x_codes = sb.tile([P, I], U32, name="x_codes", align_bytes=64)
-        x_scales = sb.tile([P, I], U8, name="x_scales", align_bytes=64)
+        x23 = sb.tile([P, 2, I], F32, name="x23")
+        lead = sb.tile([P, 2, CH, PACK], BF16, name="lead", align_bytes=64)
+        quad = sb.tile([P, 4, CH, PACK], BF16, name="quad", align_bytes=64)
+        duo = sb.tile([P, 2, P, PACK], BF16, name="duo", align_bytes=64)
+        xb = [lead[:, 0, :, :], lead[:, 1, :, :], quad[:, 1, :, :], quad[:, 2, :, :]]
+        lead_codes = sb.tile([P, HALF], U32, name="lead_codes", align_bytes=64)
+        lead_scales = sb.tile([P, HALF], U8, name="lead_scales", align_bytes=64)
+        quad_codes = sb.tile([P, 4 * CH], U32, name="quad_codes", align_bytes=64)
+        quad_scales = sb.tile([P, 4 * CH], U8, name="quad_scales", align_bytes=64)
+        duo_codes = sb.tile([P, 2 * P], U32, name="duo_codes", align_bytes=64)
+        duo_scales = sb.tile([P, 2 * P], U8, name="duo_scales", align_bytes=64)
+        x_codes = [lead_codes[:], quad_codes[:, CH : 3 * CH]]
+        x_scales = [lead_scales[:], quad_scales[:, CH : 3 * CH]]
+        w_codes = [duo_codes[:, 0:P], duo_codes[:, P:], quad_codes[:, 0:CH], quad_codes[:, 3 * CH :]]
+        w_scales = [duo_scales[:, 0:P], duo_scales[:, P:], quad_scales[:, 0:CH], quad_scales[:, 3 * CH :]]
+
+        def quantize(codes, scales, src):
+            nc.vector.quantize_mx(out=codes.bitcast(FP8X4), scales=scales, in_=src.rearrange("p e c t -> p (e c t)"))
 
         for t in range(2):
             nc.vector.tensor_tensor(x01[:, t, :], vec_t[t][:].indirect(offs_t[:]), picked[t][:], SUB)
         for c in range(NCH):
             cols = slice(c * CH, (c + 1) * CH)
             nc.scalar.activation(xb[c][:, :, 0:2], x01[:, :, cols].rearrange("p t i -> p i t"), IDENT)
-        for t in range(2, PACK):
-            for c in range(NCH):
-                cols = slice(c * CH, (c + 1) * CH)
-                nc.vector.tensor_tensor(
-                    x23[c][:, t - 2, :],
-                    vec_t[t][:].indirect(offs_t[:, c * OC : (c + 1) * OC]),
-                    picked[t][:, cols],
-                    SUB,
-                )
+        nc.vector.tensor_tensor(x23[:, 0, :], vec_t[2][:].indirect(offs_t[:]), picked[2][:], SUB)
         for c in range(NCH):
             cols = slice(c * CH, (c + 1) * CH)
-            nc.scalar.activation(xb[c][:, :, 2:4], x23[c][:].rearrange("p t i -> p i t"), IDENT)
-            nc.vector.quantize_mx(
-                out=x_codes[:, cols].bitcast(FP8X4),
-                scales=x_scales[:, cols],
-                in_=xb[c][:].rearrange("p i t -> p (i t)"),
+            nc.vector.tensor_tensor(
+                x23[:, 1, cols], vec_t[3][:].indirect(offs_t[:, c * OC : (c + 1) * OC]), picked[3][:, cols], SUB
             )
+        for c in range(NCH):
+            cols = slice(c * CH, (c + 1) * CH)
+            nc.scalar.activation(xb[c][:, :, 2:4], x23[:, :, cols].rearrange("p t i -> p i t"), IDENT)
+        quantize(lead_codes[:], lead_scales[:], lead[:])
 
-        w_codes = sb.tile([P, F], U32, name="w_codes", align_bytes=64)
-        w_scales = sb.tile([P, F], U8, name="w_scales", align_bytes=64)
-        wo_v = wo_raw[:].rearrange("p t (m j) -> p m j t", j=PACK)
-        for u in range(2):
-            wb = sb.tile([P, 2, P, PACK], BF16, name="wb%d" % u, align_bytes=64)
-            wb_v = wb[:].rearrange("p j m t -> p m j t")
+        wo_v = wo_raw[:].rearrange("p t (m j) -> p m t j", j=PACK)
+        for u, dealt in enumerate((duo[:], quad[:, 0:4:3, :, :])):
+            wb_v = dealt.rearrange("p j m t -> p m t j")
             s = WO_SPLIT[u]
-            nc.vector.tensor_copy(wb_v[:, 0:s, :, :], wo_v[:, 0:s, 2 * u : 2 * u + 2, :])
-            nc.scalar.activation(wb_v[:, s:P, :, :], wo_v[:, s:P, 2 * u : 2 * u + 2, :], IDENT)
+            nc.vector.tensor_copy(wb_v[:, 0:s, :, :], wo_v[:, 0:s, :, 2 * u : 2 * u + 2])
+            if s < P:
+                nc.scalar.activation(wb_v[:, s:P, :, :], wo_v[:, s:P, :, 2 * u : 2 * u + 2], IDENT)
             for e in range(2):
-                j = 2 * u + e
-                cols = slice(j * P, (j + 1) * P)
-                nc.vector.quantize_mx(
-                    out=w_codes[:, cols].bitcast(FP8X4),
-                    scales=w_scales[:, cols],
-                    in_=wb[:, e, :, :].rearrange("p m t -> p (m t)"),
-                )
+                if u == 1:
+                    cols = slice(e * HALF, (e + 1) * HALF)
+                    quantize(quad_codes[:, cols], quad_scales[:, cols], quad[:, 2 * e : 2 * e + 2, :, :])
+                else:
+                    quantize(w_codes[e], w_scales[e], duo[:, e : e + 1, :, :])
 
-        y_codes = sb.tile([P, I], U32, name="y_codes", align_bytes=64)
+        y = [sb.tile([P, PACK, HALF], F32, name="y%d" % h) for h in range(2)]
+        yb = [sb.tile([P, 2, CH, PACK], BF16, name="yb%d" % h, align_bytes=64) for h in range(2)]
+        y_codes = [sb.tile([P, HALF], U32, name="y_codes%d" % h, align_bytes=64) for h in range(2)]
         y_scales = sb.tile([P, I], U8, name="y_scales", align_bytes=64)
         out0_v = out_0.rearrange("(p j) i -> p j i", j=PACK)
         words_v = out_1[0].rearrange("l c r -> l (c r)").bitcast(I32)
         scales_v = out_2[0].bitcast(I32)
 
-        def quantize_y(yb, cols):
-            nc.vector.quantize_mx(
-                out=y_codes[:, cols].bitcast(FP8X4),
-                scales=y_scales[:, cols],
-                in_=yb[:].rearrange("p i j -> p (i j)"),
+        def project(j, h):
+            acc = ps.tile([P, HALF], F32, name="acc%d_%d" % (j, h))
+            nc.tensor.matmul_mx(
+                out=acc[:],
+                lhsT=w_codes[j].bitcast(FP8X4),
+                lhsT_scale=w_scales[j],
+                rhs=x_codes[h].bitcast(FP8X4),
+                rhs_scale=x_scales[h],
+                start=True,
+                stop=True,
             )
-
-        for h in range(2):
-            hc = slice(h * HALF, (h + 1) * HALF)
-            y = sb.tile([P, PACK, HALF], F32, name="y%d" % h)
-            for j in range(PACK):
-                acc = ps.tile([P, HALF], F32, name="acc%d_%d" % (h, j))
-                wc = slice(j * P, (j + 1) * P)
-                nc.tensor.matmul_mx(
-                    out=acc[:],
-                    lhsT=w_codes[:, wc].bitcast(FP8X4),
-                    lhsT_scale=w_scales[:, wc],
-                    rhs=x_codes[:, hc].bitcast(FP8X4),
-                    rhs_scale=x_scales[:, hc],
-                    start=True,
-                    stop=True,
-                )
-                if h == 0 and j % 2 == 1:
-                    nc.vector.tensor_scalar_add(y[:, j, :], acc[:], bias_t[:, j : j + 1])
-                else:
-                    nc.scalar.activation(y[:, j, :], acc[:], IDENT, bias=bias_t[:, j : j + 1])
-            nc.sync.dma_start(out0_v[:, :, hc], y[:])
-            if h == 0:
-                yb = sb.tile([P, HALF, PACK], BF16, name="yb0", align_bytes=64)
-                nc.vector.tensor_copy(
-                    yb[:].rearrange("p (c i) j -> p c j i", i=4),
-                    y[:].rearrange("p j (c i) -> p c j i", i=4),
-                )
-                quantize_y(yb, hc)
+            if h == 0 and j in (1, 2):
+                nc.vector.tensor_scalar_add(y[h][:, j, :], acc[:], bias_t[:, j : j + 1])
             else:
-                for e in range(2):
-                    yb = sb.tile([P, CH, PACK], BF16, name="yb1_%d" % e, align_bytes=64)
-                    dst = yb[:].rearrange("p (c i) j -> p c j i", i=4)
-                    src = y[:, :, e * CH : (e + 1) * CH].rearrange("p j (c i) -> p c j i", i=4)
-                    if e == 0:
-                        nc.vector.tensor_copy(dst, src)
-                    else:
-                        nc.scalar.activation(dst, src, IDENT)
-                    quantize_y(yb, slice(HALF + e * CH, HALF + (e + 1) * CH))
-            nc.sync.dma_start(words_v[:, hc], y_codes[:, hc].bitcast(I32))
+                nc.scalar.activation(y[h][:, j, :], acc[:], IDENT, bias=bias_t[:, j : j + 1])
+            if h == 0:
+                nc.sync.dma_start(out0_v[:, j, 0:HALF], y[h][:, j, :])
+            elif j % 2 == 1:
+                nc.sync.dma_start(out0_v[:, j - 1 : j + 1, h * HALF : (h + 1) * HALF], y[h][:, j - 1 : j + 1, :])
+
+        def weave_views(h, first, count):
+            dst = yb[h][:].rearrange("p e (c i) j -> p (e c) j i", i=4)
+            src = y[h][:].rearrange("p j (c i) -> p c j i", i=4)
+            groups = slice(first // 4, (first + count) // 4)
+            return dst[:, groups, :, :], src[:, groups, :, :]
+
+        def finish(h):
+            cols = slice(h * HALF, (h + 1) * HALF)
+            quantize(y_codes[h][:], y_scales[:, cols], yb[h][:])
+            nc.sync.dma_start(words_v[:, cols], y_codes[h][:].bitcast(I32))
+
+        for j in range(PACK):
+            project(j, 0)
+        nc.vector.tensor_copy(*weave_views(0, 0, HALF))
+        for j in range(PACK):
+            project(j, 1)
+        finish(0)
+        nc.vector.tensor_copy(*weave_views(1, 0, 144))
+        nc.scalar.activation(*weave_views(1, 144, HALF - 144), IDENT)
+        finish(1)
         for q in range(4):
             queue = nc.sync if q < 2 else nc.scalar
             queue.dma_start(scales_v[4 * q : 4 * q + 4, :], y_scales[32 * q : 32 * q + 4, :].bitcast(I32))

@@ -34,25 +34,27 @@ def tile_attend_pqremainder_pl_kernel(tc, vec, book, wo, bias, offs, offs2, out_
         offs_t = sb.tile([P, I // 16], U16, name="offs_t")
         offs2_t = sb.tile([P, I // 16], U16, name="offs2_t")
         bias_t = sb.tile([P, PACK], F32, name="bias_t")
-        book_t = [sb.tile([P, C], F32, name="book%d" % t) for t in range(PACK)]
+        book_pair = [sb.tile([P, 2 * C], F32, name="book_pair%d" % u) for u in range(2)]
+        book_odd = [sb.tile([P, C], F32, name="book_odd%d" % u) for u in range(2)]
         vec_t = [sb.tile([P, T], F32, name="vec%d" % t) for t in range(PACK)]
         wo_raw = sb.tile([P, PACK, F], F32, name="wo_raw")
 
-        book_v = book.rearrange("(p t) c -> p t c", t=PACK)
+        book_v = book.rearrange("(p u e) c -> p u (e c)", u=2, e=2)
         vec_v = vec.rearrange("(p t) c -> p t c", t=PACK)
-        nc.sync.dma_start(book_t[0][:], book_v[:, 0, :])
+        nc.sync.dma_start(book_pair[0][:], book_v[:, 0, :])
         nc.sync.dma_start(offs2_t[:], offs2)
         nc.sync.dma_start(offs_t[:], offs)
-        for t in range(1, PACK):
-            nc.sync.dma_start(book_t[t][:], book_v[:, t, :])
+        nc.sync.dma_start(book_pair[1][:], book_v[:, 1, :])
         for t in range(PACK):
             nc.sync.dma_start(vec_t[t][:], vec_v[:, t, :])
         nc.sync.dma_start(wo_raw[:], wo.rearrange("(p t) f -> p t f", t=PACK))
         nc.sync.dma_start(bias_t[:], bias.rearrange("(p j) o -> p (j o)", j=PACK))
 
         picked = [sb.tile([P, I], F32, name="picked%d" % t) for t in range(PACK)]
-        for t in range(PACK):
-            nc.vector.tensor_copy(picked[t][:], book_t[t][:].indirect(offs2_t[:]))
+        for u in range(2):
+            nc.scalar.activation(book_odd[u][:], book_pair[u][:, C:], IDENT)
+            nc.vector.tensor_copy(picked[2 * u][:], book_pair[u][:].indirect(offs2_t[:]))
+            nc.vector.tensor_copy(picked[2 * u + 1][:], book_odd[u][:].indirect(offs2_t[:]))
 
         x01 = sb.tile([P, 2, I], F32, name="x01")
         x23 = sb.tile([P, 2, I], F32, name="x23")

@@ -114,25 +114,39 @@ def tile_attend_pqremainder_pl_kernel(tc, vec, book, wo, bias, offs, offs2, out_
         words_v = out_1[0].rearrange("l c r -> l (c r)").bitcast(I32)
         scales_v = out_2[0].bitcast(I32)
 
-        def project(j, h):
-            acc = ps.tile([P, HALF], F32, name="acc%d_%d" % (j, h))
+        def multiply(acc, j, h, first, count):
             nc.tensor.matmul_mx(
-                out=acc[:],
+                out=acc,
                 lhsT=w_codes[j].bitcast(FP8X4),
                 lhsT_scale=w_scales[j],
-                rhs=x_codes[h].bitcast(FP8X4),
-                rhs_scale=x_scales[h],
+                rhs=x_codes[h][:, first : first + count].bitcast(FP8X4),
+                rhs_scale=x_scales[h][:, first : first + count],
                 start=True,
                 stop=True,
             )
-            if h == 0 and j in (1, 2):
-                nc.vector.tensor_scalar_add(y[h][:, j, :], acc[:], bias_t[:, j : j + 1])
-            else:
-                nc.scalar.activation(y[h][:, j, :], acc[:], IDENT, bias=bias_t[:, j : j + 1])
+
+        def project(h):
+            cols = slice(h * HALF, (h + 1) * HALF)
+            for j in range(2 if h == 0 else PACK):
+                pieces = ((0, CH), (CH, CH)) if (j, h) == (PACK - 1, 1) else ((0, HALF),)
+                for first, count in pieces:
+                    tag = "acc0_0" if first else "acc%d_%d" % (j, h)
+                    acc = ps.tile([P, count], F32, name="acc", tag=tag)
+                    multiply(acc[:], j, h, first, count)
+                    dst = y[h][:, j, first : first + count]
+                    nc.scalar.activation(dst, acc[:], IDENT, bias=bias_t[:, j : j + 1])
+                if h == 0:
+                    nc.sync.dma_start(out0_v[:, j, cols], y[h][:, j, :])
+                elif j % 2 == 1:
+                    nc.sync.dma_start(out0_v[:, j - 1 : j + 1, cols], y[h][:, j - 1 : j + 1, :])
             if h == 0:
-                nc.sync.dma_start(out0_v[:, j, 0:HALF], y[h][:, j, :])
-            elif j % 2 == 1:
-                nc.sync.dma_start(out0_v[:, j - 1 : j + 1, h * HALF : (h + 1) * HALF], y[h][:, j - 1 : j + 1, :])
+                for first in (0, CH):
+                    acc = ps.tile([P, 2, CH], F32, name="pair%d" % first)
+                    for e in range(2):
+                        multiply(acc[:, e, :], 2 + e, h, first, CH)
+                    dst = y[h][:, 2:4, first : first + CH]
+                    nc.vector.tensor_tensor(dst, acc[:], bias_t[:, 2:4].unsqueeze(2).to_broadcast([P, 2, CH]), ADD)
+                nc.sync.dma_start(out0_v[:, 2:4, cols], y[h][:, 2:4, :])
 
         def weave_views(h, first, count):
             dst = yb[h][:].rearrange("p e (c i) j -> p (e c) j i", i=4)
@@ -140,20 +154,29 @@ def tile_attend_pqremainder_pl_kernel(tc, vec, book, wo, bias, offs, offs2, out_
             groups = slice(first // 4, (first + count) // 4)
             return dst[:, groups, :, :], src[:, groups, :, :]
 
-        def finish(h):
-            cols = slice(h * HALF, (h + 1) * HALF)
-            quantize(y_codes[h][:], y_scales[:, cols], yb[h][:])
-            nc.sync.dma_start(words_v[:, cols], y_codes[h][:].bitcast(I32))
+        def quantize_y(h, first, count):
+            lo = h * HALF + first
+            nc.vector.quantize_mx(
+                out=y_codes[h][:, first : first + count].bitcast(FP8X4),
+                scales=y_scales[:, lo : lo + count],
+                in_=yb[h][:].rearrange("p e c t -> p (e c t)")[:, PACK * first : PACK * (first + count)],
+            )
 
-        for j in range(PACK):
-            project(j, 0)
-        nc.vector.tensor_copy(*weave_views(0, 0, HALF))
-        for j in range(PACK):
-            project(j, 1)
-        finish(0)
-        nc.vector.tensor_copy(*weave_views(1, 0, 144))
-        nc.scalar.activation(*weave_views(1, 144, HALF - 144), IDENT)
-        finish(1)
+        def store_words(h):
+            nc.sync.dma_start(words_v[:, h * HALF : (h + 1) * HALF], y_codes[h][:].bitcast(I32))
+
+        project(0)
+        for first in (0, CH):
+            nc.vector.tensor_copy(*weave_views(0, first, CH))
+        for first in (0, CH):
+            quantize_y(0, first, CH)
+        project(1)
+        store_words(0)
+        nc.vector.tensor_copy(*weave_views(1, 0, CH))
+        nc.vector.tensor_copy(*weave_views(1, CH, 64))
+        nc.scalar.activation(*weave_views(1, CH + 64, 64), IDENT)
+        for first in (0, CH):
+            quantize_y(1, first, CH)
+        store_words(1)
         for q in range(4):
-            queue = nc.sync if q < 2 else nc.scalar
-            queue.dma_start(scales_v[4 * q : 4 * q + 4, :], y_scales[32 * q : 32 * q + 4, :].bitcast(I32))
+            nc.scalar.dma_start(scales_v[4 * q : 4 * q + 4, :], y_scales[32 * q : 32 * q + 4, :].bitcast(I32))

@@ -128,16 +128,16 @@ def tile_attend_pqremainder_pl_kernel(tc, vec, book, wo, bias, offs, offs2, out_
         def project(h):
             cols = slice(h * HALF, (h + 1) * HALF)
             for j in range(2 if h == 0 else PACK):
-                pieces = ((0, CH), (CH, CH)) if (j, h) == (PACK - 1, 1) else ((0, HALF),)
+                pieces = ((0, CH), (CH, CH)) if (j, h) in ((0, 0), (PACK - 1, 1)) else ((0, HALF),)
                 for first, count in pieces:
-                    tag = "acc0_0" if first else "acc%d_%d" % (j, h)
+                    tag = "acc0_0_%d" % first if (j, h) == (PACK - 1, 1) else "acc%d_%d_%d" % (j, h, first)
                     acc = ps.tile([P, count], F32, name="acc", tag=tag)
                     multiply(acc[:], j, h, first, count)
                     dst = y[h][:, j, first : first + count]
                     nc.scalar.activation(dst, acc[:], IDENT, bias=bias_t[:, j : j + 1])
-                if h == 0:
-                    nc.sync.dma_start(out0_v[:, j, cols], y[h][:, j, :])
-                elif j % 2 == 1:
+                    if h == 0:
+                        nc.sync.dma_start(out0_v[:, j, first : first + count], dst)
+                if h == 1 and j % 2 == 1:
                     nc.sync.dma_start(out0_v[:, j - 1 : j + 1, cols], y[h][:, j - 1 : j + 1, :])
             if h == 0:
                 for first in (0, CH):

@@ -22,7 +22,7 @@ CH = 128
 NCH = I // CH
 OC = CH // 16
 HALF = 256
-WO_SPLIT = (128, 64)
+WO_SPLIT = (92, 64)
 
 
 def tile_attend_pqremainder_pl_kernel(tc, vec, book, wo, bias, offs, offs2, out_0, out_1, out_2):
@@ -37,7 +37,7 @@ def tile_attend_pqremainder_pl_kernel(tc, vec, book, wo, bias, offs, offs2, out_
         book_pair = [sb.tile([P, 2 * C], F32, name="book_pair%d" % u) for u in range(2)]
         book_odd = [sb.tile([P, C], F32, name="book_odd%d" % u) for u in range(2)]
         vec_t = [sb.tile([P, T], F32, name="vec%d" % t) for t in range(PACK)]
-        wo_raw = sb.tile([P, PACK, F], F32, name="wo_raw")
+        wo_raw = sb.tile([P, PACK, F], F32, name="wo_raw", tag="wo_slot", align_bytes=64)
 
         book_v = book.rearrange("(p u e) c -> p u (e c)", u=2, e=2)
         vec_v = vec.rearrange("(p t) c -> p t c", t=PACK)
@@ -59,19 +59,16 @@ def tile_attend_pqremainder_pl_kernel(tc, vec, book, wo, bias, offs, offs2, out_
         x01 = sb.tile([P, 2, I], F32, name="x01")
         x23 = sb.tile([P, 2, I], F32, name="x23")
         lead = sb.tile([P, 2, CH, PACK], BF16, name="lead", align_bytes=64)
-        quad = sb.tile([P, 4, CH, PACK], BF16, name="quad", align_bytes=64)
-        duo = sb.tile([P, 2, P, PACK], BF16, name="duo", align_bytes=64)
-        xb = [lead[:, 0, :, :], lead[:, 1, :, :], quad[:, 1, :, :], quad[:, 2, :, :]]
+        late = sb.tile([P, 2, CH, PACK], BF16, name="late", align_bytes=64)
+        wb = [sb.tile([P, 2, P, PACK], BF16, name="wb%d" % u, align_bytes=64) for u in range(2)]
+        xb = [lead[:, 0, :, :], lead[:, 1, :, :], late[:, 0, :, :], late[:, 1, :, :]]
         lead_codes = sb.tile([P, HALF], U32, name="lead_codes", align_bytes=64)
         lead_scales = sb.tile([P, HALF], U8, name="lead_scales", align_bytes=64)
-        quad_codes = sb.tile([P, 4 * CH], U32, name="quad_codes", align_bytes=64)
-        quad_scales = sb.tile([P, 4 * CH], U8, name="quad_scales", align_bytes=64)
-        duo_codes = sb.tile([P, 2 * P], U32, name="duo_codes", align_bytes=64)
-        duo_scales = sb.tile([P, 2 * P], U8, name="duo_scales", align_bytes=64)
-        x_codes = [lead_codes[:], quad_codes[:, CH : 3 * CH]]
-        x_scales = [lead_scales[:], quad_scales[:, CH : 3 * CH]]
-        w_codes = [duo_codes[:, 0:P], duo_codes[:, P:], quad_codes[:, 0:CH], quad_codes[:, 3 * CH :]]
-        w_scales = [duo_scales[:, 0:P], duo_scales[:, P:], quad_scales[:, 0:CH], quad_scales[:, 3 * CH :]]
+        late_scales = sb.tile([P, HALF], U8, name="late_scales", align_bytes=64)
+        wq_codes = sb.tile([P, PACK * P], U32, name="wq_codes", align_bytes=64)
+        wq_scales = sb.tile([P, PACK * P], U8, name="wq_scales", align_bytes=64)
+        w_codes = [wq_codes[:, j * P : (j + 1) * P] for j in range(PACK)]
+        w_scales = [wq_scales[:, j * P : (j + 1) * P] for j in range(PACK)]
 
         def quantize(codes, scales, src):
             nc.vector.quantize_mx(out=codes.bitcast(FP8X4), scales=scales, in_=src.rearrange("p e c t -> p (e c t)"))
@@ -89,22 +86,28 @@ def tile_attend_pqremainder_pl_kernel(tc, vec, book, wo, bias, offs, offs2, out_
             )
         for c in range(NCH):
             cols = slice(c * CH, (c + 1) * CH)
-            nc.scalar.activation(xb[c][:, :, 2:4], x23[:, :, cols].rearrange("p t i -> p i t"), IDENT)
+            src = x23[:, :, cols].rearrange("p t i -> p i t")
+            if c == 2:
+                nc.vector.tensor_copy(xb[c][:, :, 2:4], src)
+            else:
+                nc.scalar.activation(xb[c][:, :, 2:4], src, IDENT)
         quantize(lead_codes[:], lead_scales[:], lead[:])
 
         wo_v = wo_raw[:].rearrange("p t (m j) -> p m t j", j=PACK)
-        for u, dealt in enumerate((duo[:], quad[:, 0:4:3, :, :])):
-            wb_v = dealt.rearrange("p j m t -> p m t j")
+        for u in range(2):
+            wb_v = wb[u][:].rearrange("p j m t -> p m t j")
             s = WO_SPLIT[u]
             nc.vector.tensor_copy(wb_v[:, 0:s, :, :], wo_v[:, 0:s, :, 2 * u : 2 * u + 2])
-            if s < P:
-                nc.scalar.activation(wb_v[:, s:P, :, :], wo_v[:, s:P, :, 2 * u : 2 * u + 2], IDENT)
-            for e in range(2):
-                if u == 1:
-                    cols = slice(e * HALF, (e + 1) * HALF)
-                    quantize(quad_codes[:, cols], quad_scales[:, cols], quad[:, 2 * e : 2 * e + 2, :, :])
-                else:
-                    quantize(w_codes[e], w_scales[e], duo[:, e : e + 1, :, :])
+            nc.scalar.activation(wb_v[:, s:P, :, :], wo_v[:, s:P, :, 2 * u : 2 * u + 2], IDENT)
+            if u == 0:
+                for e in range(2):
+                    quantize(w_codes[e], w_scales[e], wb[0][:, e : e + 1, :, :])
+            else:
+                quantize(wq_codes[:, 2 * P :], wq_scales[:, 2 * P :], wb[1][:])
+        late_codes = sb.tile([P, HALF], U32, name="late_codes", tag="wo_slot", align_bytes=64)
+        quantize(late_codes[:], late_scales[:], late[:])
+        x_codes = [lead_codes[:], late_codes[:]]
+        x_scales = [lead_scales[:], late_scales[:]]
 
         y = [sb.tile([P, PACK, HALF], F32, name="y%d" % h) for h in range(2)]
         yb = [sb.tile([P, 2, CH, PACK], BF16, name="yb%d" % h, align_bytes=64) for h in range(2)]

@@ -15,14 +15,13 @@ FP8X4 = mybir.dt.float8_e4m3fn_x4
 SUB = mybir.AluOpType.subtract
 ADD = mybir.AluOpType.add
 IDENT = mybir.ActivationFunctionType.Identity
+COPY = mybir.ActivationFunctionType.Copy
 
 P = 128
 PACK = 4
 CH = 128
-NCH = I // CH
-OC = CH // 16
 HALF = 256
-WO_SPLIT = (92, 64)
+WO_SPLIT = (84, 36, 72)
 
 
 def tile_attend_pqremainder_pl_kernel(tc, vec, book, wo, bias, offs, offs2, out_0, out_1, out_2):
@@ -34,83 +33,108 @@ def tile_attend_pqremainder_pl_kernel(tc, vec, book, wo, bias, offs, offs2, out_
         offs_t = sb.tile([P, I // 16], U16, name="offs_t")
         offs2_t = sb.tile([P, I // 16], U16, name="offs2_t")
         bias_t = sb.tile([P, PACK], F32, name="bias_t")
-        book_pair = [sb.tile([P, 2 * C], F32, name="book_pair%d" % u) for u in range(2)]
-        book_odd = [sb.tile([P, C], F32, name="book_odd%d" % u) for u in range(2)]
-        vec_t = [sb.tile([P, T], F32, name="vec%d" % t) for t in range(PACK)]
-        wo_raw = sb.tile([P, PACK, F], F32, name="wo_raw", tag="wo_slot", align_bytes=64)
+        book_raw = sb.tile([P, PACK * C], F32, name="book_raw")
+        book_t = [sb.tile([P, C], F32, name="book%d" % t) for t in range(PACK)]
+        vec01 = sb.tile([P, 2 * T], F32, name="vec01")
+        vec_t = {t: sb.tile([P, T], F32, name="vec%d" % t) for t in (2, 3)}
+        wo_raw = sb.tile([P, PACK, F], F32, name="wo_raw")
 
-        book_v = book.rearrange("(p u e) c -> p u (e c)", u=2, e=2)
         vec_v = vec.rearrange("(p t) c -> p t c", t=PACK)
-        nc.sync.dma_start(book_pair[0][:], book_v[:, 0, :])
+        nc.sync.dma_start(book_raw[:], book.rearrange("(p t) c -> p (t c)", t=PACK))
         nc.sync.dma_start(offs2_t[:], offs2)
         nc.sync.dma_start(offs_t[:], offs)
-        nc.sync.dma_start(book_pair[1][:], book_v[:, 1, :])
-        for t in range(PACK):
+        nc.sync.dma_start(vec01[:], vec.rearrange("(p u e) c -> p u (e c)", u=2, e=2)[:, 0, :])
+        for t in (2, 3):
             nc.sync.dma_start(vec_t[t][:], vec_v[:, t, :])
         nc.sync.dma_start(wo_raw[:], wo.rearrange("(p t) f -> p t f", t=PACK))
         nc.sync.dma_start(bias_t[:], bias.rearrange("(p j) o -> p (j o)", j=PACK))
 
-        picked = [sb.tile([P, I], F32, name="picked%d" % t) for t in range(PACK)]
+        def listed(first, count):
+            return offs_t[:, first // 16 : (first + count) // 16]
+
+        picked = [sb.tile([P, 2, I], F32, name="picked%d" % u) for u in range(2)]
         for u in range(2):
-            nc.scalar.activation(book_odd[u][:], book_pair[u][:, C:], IDENT)
-            nc.vector.tensor_copy(picked[2 * u][:], book_pair[u][:].indirect(offs2_t[:]))
-            nc.vector.tensor_copy(picked[2 * u + 1][:], book_odd[u][:].indirect(offs2_t[:]))
+            even, odd = 2 * u, 2 * u + 1
+            nc.vector.tensor_copy(book_t[even][:], book_raw[:, even * C : (even + 1) * C])
+            nc.vector.tensor_copy(picked[u][:, 0, :], book_t[even][:].indirect(offs2_t[:]))
+            nc.scalar.activation(book_t[odd][:], book_raw[:, odd * C : (odd + 1) * C], IDENT)
+            nc.scalar.activation(picked[u][:, 1, :], book_t[odd][:].indirect(offs2_t[:]), COPY)
 
         x01 = sb.tile([P, 2, I], F32, name="x01")
-        x23 = sb.tile([P, 2, I], F32, name="x23")
-        lead = sb.tile([P, 2, CH, PACK], BF16, name="lead", align_bytes=64)
-        late = sb.tile([P, 2, CH, PACK], BF16, name="late", align_bytes=64)
-        wb = [sb.tile([P, 2, P, PACK], BF16, name="wb%d" % u, align_bytes=64) for u in range(2)]
-        xb = [lead[:, 0, :, :], lead[:, 1, :, :], late[:, 0, :, :], late[:, 1, :, :]]
-        lead_codes = sb.tile([P, HALF], U32, name="lead_codes", align_bytes=64)
-        lead_scales = sb.tile([P, HALF], U8, name="lead_scales", align_bytes=64)
-        late_scales = sb.tile([P, HALF], U8, name="late_scales", align_bytes=64)
+        v23 = sb.tile([P, 2, HALF], F32, name="v23")
+        x23 = sb.tile([P, 2, HALF], F32, name="x23")
+        xb = [sb.tile([P, HALF, PACK], BF16, name="xb%d" % h, align_bytes=64) for h in range(2)]
+        x_codes = [sb.tile([P, HALF], U32, name="lead_codes", align_bytes=64)]
+        x_scales = [sb.tile([P, HALF], U8, name="x_scales%d" % h, align_bytes=64) for h in range(2)]
+        wb = [sb.tile([P, 2, P, PACK], BF16, name="wb%d" % u, tag="wb%d" % u, align_bytes=64) for u in range(2)]
         wq_codes = sb.tile([P, PACK * P], U32, name="wq_codes", align_bytes=64)
         wq_scales = sb.tile([P, PACK * P], U8, name="wq_scales", align_bytes=64)
         w_codes = [wq_codes[:, j * P : (j + 1) * P] for j in range(PACK)]
         w_scales = [wq_scales[:, j * P : (j + 1) * P] for j in range(PACK)]
 
-        def quantize(codes, scales, src):
-            nc.vector.quantize_mx(out=codes.bitcast(FP8X4), scales=scales, in_=src.rearrange("p e c t -> p (e c t)"))
+        v1 = sb.tile([P, I], F32, name="v1")
+        nc.vector.tensor_tensor(x01[:, 0, :], vec01[:].indirect(offs_t[:]), picked[0][:, 0, :], SUB)
+        nc.scalar.activation(v1[:], vec01[:, T:].indirect(offs_t[:]), COPY)
+        nc.vector.tensor_tensor(x01[:, 1, :], v1[:], picked[0][:, 1, :], SUB)
+        for h in range(2):
+            cols = slice(h * HALF, (h + 1) * HALF)
+            nc.scalar.activation(xb[h][:, :, 0:2], x01[:, :, cols].rearrange("p t i -> p i t"), IDENT)
 
-        for t in range(2):
-            nc.vector.tensor_tensor(x01[:, t, :], vec_t[t][:].indirect(offs_t[:]), picked[t][:], SUB)
-        for c in range(NCH):
-            cols = slice(c * CH, (c + 1) * CH)
-            nc.scalar.activation(xb[c][:, :, 0:2], x01[:, :, cols].rearrange("p t i -> p i t"), IDENT)
-        nc.vector.tensor_tensor(x23[:, 0, :], vec_t[2][:].indirect(offs_t[:]), picked[2][:], SUB)
-        for c in range(NCH):
-            cols = slice(c * CH, (c + 1) * CH)
+        nc.vector.tensor_copy(v23[:, 0, :], vec_t[2][:].indirect(listed(0, HALF)))
+        nc.vector.tensor_tensor(x23[:, 0, :], vec_t[2][:].indirect(listed(HALF, HALF)), picked[1][:, 0, HALF:], SUB)
+        for first in (0, CH):
+            cols = slice(first, first + CH)
+            nc.scalar.activation(v23[:, 1, cols], vec_t[3][:].indirect(listed(first, CH)), COPY)
             nc.vector.tensor_tensor(
-                x23[:, 1, cols], vec_t[3][:].indirect(offs_t[:, c * OC : (c + 1) * OC]), picked[3][:, cols], SUB
+                x23[:, 1, cols],
+                vec_t[3][:].indirect(listed(HALF + first, CH)),
+                picked[1][:, 1, HALF + first : HALF + first + CH],
+                SUB,
             )
-        for c in range(NCH):
-            cols = slice(c * CH, (c + 1) * CH)
-            src = x23[:, :, cols].rearrange("p t i -> p i t")
-            if c == 2:
-                nc.vector.tensor_copy(xb[c][:, :, 2:4], src)
-            else:
-                nc.scalar.activation(xb[c][:, :, 2:4], src, IDENT)
-        quantize(lead_codes[:], lead_scales[:], lead[:])
+        for first in (0, CH):
+            cols = slice(first, first + CH)
+            nc.vector.tensor_tensor(
+                xb[0][:, cols, 2:4],
+                v23[:, :, cols].rearrange("p t i -> p i t"),
+                picked[1][:, :, cols].rearrange("p t i -> p i t"),
+                SUB,
+            )
+            nc.scalar.activation(xb[1][:, cols, 2:4], x23[:, :, cols].rearrange("p t i -> p i t"), IDENT)
+
+        def quantize_x(h):
+            nc.vector.quantize_mx(
+                out=x_codes[h][:].bitcast(FP8X4), scales=x_scales[h][:], in_=xb[h][:].rearrange("p c t -> p (c t)")
+            )
+
+        quantize_x(0)
+
+        def quantize_wo(first, count):
+            u, e = divmod(first, 2)
+            nc.vector.quantize_mx(
+                out=wq_codes[:, first * P : (first + count) * P].bitcast(FP8X4),
+                scales=wq_scales[:, first * P : (first + count) * P],
+                in_=wb[u][:, e : e + count, :, :].rearrange("p e m t -> p (e m t)"),
+            )
 
         wo_v = wo_raw[:].rearrange("p t (m j) -> p m t j", j=PACK)
-        for u in range(2):
-            wb_v = wb[u][:].rearrange("p j m t -> p m t j")
-            s = WO_SPLIT[u]
-            nc.vector.tensor_copy(wb_v[:, 0:s, :, :], wo_v[:, 0:s, :, 2 * u : 2 * u + 2])
-            nc.scalar.activation(wb_v[:, s:P, :, :], wo_v[:, s:P, :, 2 * u : 2 * u + 2], IDENT)
-            if u == 0:
-                for e in range(2):
-                    quantize(w_codes[e], w_scales[e], wb[0][:, e : e + 1, :, :])
-            else:
-                quantize(wq_codes[:, 2 * P :], wq_scales[:, 2 * P :], wb[1][:])
-        late_codes = sb.tile([P, HALF], U32, name="late_codes", tag="wo_slot", align_bytes=64)
-        quantize(late_codes[:], late_scales[:], late[:])
-        x_codes = [lead_codes[:], late_codes[:]]
-        x_scales = [lead_scales[:], late_scales[:]]
+
+        def round_wo(u, lo, hi):
+            return wb[u][:].rearrange("p j m t -> p m t j")[:, lo:hi, :, :], wo_v[:, lo:hi, :, 2 * u : 2 * u + 2]
+
+        nc.vector.tensor_copy(*round_wo(0, 0, WO_SPLIT[0]))
+        nc.scalar.activation(*round_wo(0, WO_SPLIT[0], P), IDENT)
+        nc.vector.tensor_copy(*round_wo(1, 0, WO_SPLIT[1]))
+        nc.scalar.activation(*round_wo(1, WO_SPLIT[2], P), IDENT)
+        quantize_wo(0, 1)
+        quantize_wo(1, 1)
+        nc.vector.tensor_copy(*round_wo(1, WO_SPLIT[1], WO_SPLIT[2]))
+        quantize_wo(2, 1)
+        quantize_wo(3, 1)
+        x_codes.append(sb.tile([P, HALF], U32, name="late_codes", tag="wb1", align_bytes=64))
+        quantize_x(1)
 
         y = [sb.tile([P, PACK, HALF], F32, name="y%d" % h) for h in range(2)]
-        yb = [sb.tile([P, 2, CH, PACK], BF16, name="yb%d" % h, align_bytes=64) for h in range(2)]
+        yb = {}
         y_codes = [sb.tile([P, HALF], U32, name="y_codes%d" % h, align_bytes=64) for h in range(2)]
         y_scales = sb.tile([P, I], U8, name="y_scales", align_bytes=64)
         out0_v = out_0.rearrange("(p j) i -> p j i", j=PACK)
@@ -128,56 +152,71 @@ def tile_attend_pqremainder_pl_kernel(tc, vec, book, wo, bias, offs, offs2, out_
                 stop=True,
             )
 
-        def project(h):
-            cols = slice(h * HALF, (h + 1) * HALF)
-            for j in range(2 if h == 0 else PACK):
-                pieces = ((0, CH), (CH, CH)) if (j, h) in ((0, 0), (PACK - 1, 1)) else ((0, HALF),)
-                for first, count in pieces:
-                    tag = "acc0_0_%d" % first if (j, h) == (PACK - 1, 1) else "acc%d_%d_%d" % (j, h, first)
-                    acc = ps.tile([P, count], F32, name="acc", tag=tag)
-                    multiply(acc[:], j, h, first, count)
-                    dst = y[h][:, j, first : first + count]
-                    nc.scalar.activation(dst, acc[:], IDENT, bias=bias_t[:, j : j + 1])
-                    if h == 0:
-                        nc.sync.dma_start(out0_v[:, j, first : first + count], dst)
-                if h == 1 and j % 2 == 1:
-                    nc.sync.dma_start(out0_v[:, j - 1 : j + 1, cols], y[h][:, j - 1 : j + 1, :])
-            if h == 0:
-                for first in (0, CH):
-                    acc = ps.tile([P, 2, CH], F32, name="pair%d" % first)
-                    for e in range(2):
-                        multiply(acc[:, e, :], 2 + e, h, first, CH)
-                    dst = y[h][:, 2:4, first : first + CH]
-                    nc.vector.tensor_tensor(dst, acc[:], bias_t[:, 2:4].unsqueeze(2).to_broadcast([P, 2, CH]), ADD)
-                nc.sync.dma_start(out0_v[:, 2:4, cols], y[h][:, 2:4, :])
+        def project(j, h, first, count, bank):
+            acc = ps.tile([P, count], F32, name="acc", tag=bank)
+            multiply(acc[:], j, h, first, count)
+            nc.scalar.activation(y[h][:, j, first : first + count], acc[:], IDENT, bias=bias_t[:, j : j + 1])
+
+        def project_pair(h, first, bank):
+            acc = ps.tile([P, 2, CH], F32, name="pair", tag=bank)
+            for e in range(2):
+                multiply(acc[:, e, :], 2 + e, h, first, CH)
+            nc.vector.tensor_tensor(
+                y[h][:, 2:4, first : first + CH], acc[:], bias_t[:, 2:4].unsqueeze(2).to_broadcast([P, 2, CH]), ADD
+            )
+
+        def project_on_vector(j, h, first, count, bank):
+            acc = ps.tile([P, count], F32, name="acc", tag=bank)
+            multiply(acc[:], j, h, first, count)
+            nc.vector.tensor_scalar_add(y[h][:, j, first : first + count], acc[:], bias_t[:, j : j + 1])
+
+        def store_rows(h, j, rows, first, count):
+            lo = h * HALF + first
+            nc.sync.dma_start(out0_v[:, j : j + rows, lo : lo + count], y[h][:, j : j + rows, first : first + count])
 
         def weave_views(h, first, count):
-            dst = yb[h][:].rearrange("p e (c i) j -> p (e c) j i", i=4)
+            chunk, inside = divmod(h * HALF + first, CH)
+            if chunk not in yb:
+                yb[chunk] = sb.tile([P, CH, PACK], BF16, name="yb", tag="yb%d" % (0, 1, 0, 3)[chunk], align_bytes=64)
+            dst = yb[chunk][:].rearrange("p (c i) j -> p c j i", i=4)
             src = y[h][:].rearrange("p j (c i) -> p c j i", i=4)
-            groups = slice(first // 4, (first + count) // 4)
-            return dst[:, groups, :, :], src[:, groups, :, :]
+            return dst[:, inside // 4 : (inside + count) // 4, :, :], src[:, first // 4 : (first + count) // 4, :, :]
 
         def quantize_y(h, first, count):
             lo = h * HALF + first
             nc.vector.quantize_mx(
                 out=y_codes[h][:, first : first + count].bitcast(FP8X4),
                 scales=y_scales[:, lo : lo + count],
-                in_=yb[h][:].rearrange("p e c t -> p (e c t)")[:, PACK * first : PACK * (first + count)],
+                in_=yb[lo // CH][:].rearrange("p c t -> p (c t)"),
             )
 
         def store_words(h):
             nc.sync.dma_start(words_v[:, h * HALF : (h + 1) * HALF], y_codes[h][:].bitcast(I32))
 
-        project(0)
+        for j in range(2):
+            project(j, 0, 0, HALF, "bank%d" % j)
+            store_rows(0, j, 1, 0, HALF)
+        for first in (0, CH):
+            project(2, 0, first, CH, "bank%d" % (2 + 2 * (first // CH)))
+            project_on_vector(3, 0, first, CH, "bank%d" % (3 + 2 * (first // CH)))
+        store_rows(0, 2, 1, 0, HALF)
+        store_rows(0, 3, 1, 0, HALF)
         for first in (0, CH):
             nc.vector.tensor_copy(*weave_views(0, first, CH))
+        project(0, 1, 0, HALF, "bank6")
+        project(1, 1, 0, HALF, "bank7")
+        store_rows(1, 0, 2, 0, HALF)
+        project(2, 1, 0, CH, "bank0")
+        project(3, 1, 0, CH, "bank1")
         for first in (0, CH):
             quantize_y(0, first, CH)
-        project(1)
         store_words(0)
-        nc.vector.tensor_copy(*weave_views(1, 0, CH))
-        nc.vector.tensor_copy(*weave_views(1, CH, 64))
-        nc.scalar.activation(*weave_views(1, CH + 64, 64), IDENT)
+        project_on_vector(2, 1, CH, CH, "bank4")
+        project(3, 1, CH, CH, "bank5")
+        store_rows(1, 2, 2, 0, HALF)
+        nc.vector.tensor_copy(*weave_views(1, 0, 56))
+        nc.vector.tensor_copy(*weave_views(1, CH, CH))
+        nc.scalar.activation(*weave_views(1, 56, 72), IDENT)
         for first in (0, CH):
             quantize_y(1, first, CH)
         store_words(1)

@@ -168,7 +168,9 @@ def tile_attend_pqremainder_pl_kernel(tc, vec, book, wo, bias, offs, offs2, out_
         def project_on_vector(j, h, first, count, bank):
             acc = ps.tile([P, count], F32, name="acc", tag=bank)
             multiply(acc[:], j, h, first, count)
-            nc.vector.tensor_scalar_add(y[h][:, j, first : first + count], acc[:], bias_t[:, j : j + 1])
+            nc.vector.tensor_tensor(
+                y[h][:, j, first : first + count], acc[:], bias_t[:, j : j + 1].to_broadcast([P, count]), ADD
+            )
 
         def store_rows(h, j, rows, first, count):
             lo = h * HALF + first

@@ -37,7 +37,7 @@ def tile_attend_pqremainder_pl_kernel(tc, vec, book, wo, bias, offs, offs2, out_
         book_t = [sb.tile([P, C], F32, name="book%d" % t) for t in range(PACK)]
         vec01 = sb.tile([P, 2 * T], F32, name="vec01")
         vec_t = {t: sb.tile([P, T], F32, name="vec%d" % t) for t in (2, 3)}
-        wo_raw = sb.tile([P, PACK, F], F32, name="wo_raw")
+        wo_raw = sb.tile([P, PACK, F], F32, name="wo_raw", tag="wo_slot", align_bytes=64)
 
         vec_v = vec.rearrange("(p t) c -> p t c", t=PACK)
         nc.sync.dma_start(book_raw[:], book.rearrange("(p t) c -> p (t c)", t=PACK))
@@ -61,8 +61,7 @@ def tile_attend_pqremainder_pl_kernel(tc, vec, book, wo, bias, offs, offs2, out_
             nc.scalar.activation(picked[u][:, 1, :], book_t[odd][:].indirect(offs2_t[:]), COPY)
 
         x01 = sb.tile([P, 2, I], F32, name="x01")
-        v23 = sb.tile([P, 2, HALF], F32, name="v23")
-        x23 = sb.tile([P, 2, HALF], F32, name="x23")
+        x23 = sb.tile([P, 2, I], F32, name="x23")
         xb = [sb.tile([P, HALF, PACK], BF16, name="xb%d" % h, align_bytes=64) for h in range(2)]
         x_codes = [sb.tile([P, HALF], U32, name="lead_codes", align_bytes=64)]
         x_scales = [sb.tile([P, HALF], U8, name="x_scales%d" % h, align_bytes=64) for h in range(2)]
@@ -76,30 +75,22 @@ def tile_attend_pqremainder_pl_kernel(tc, vec, book, wo, bias, offs, offs2, out_
         nc.vector.tensor_tensor(x01[:, 0, :], vec01[:].indirect(offs_t[:]), picked[0][:, 0, :], SUB)
         nc.scalar.activation(v1[:], vec01[:, T:].indirect(offs_t[:]), COPY)
         nc.vector.tensor_tensor(x01[:, 1, :], v1[:], picked[0][:, 1, :], SUB)
-        for h in range(2):
-            cols = slice(h * HALF, (h + 1) * HALF)
-            nc.scalar.activation(xb[h][:, :, 0:2], x01[:, :, cols].rearrange("p t i -> p i t"), IDENT)
+        nc.vector.tensor_tensor(x23[:, 0, :], vec_t[2][:].indirect(offs_t[:]), picked[1][:, 0, :], SUB)
 
-        nc.vector.tensor_copy(v23[:, 0, :], vec_t[2][:].indirect(listed(0, HALF)))
-        nc.vector.tensor_tensor(x23[:, 0, :], vec_t[2][:].indirect(listed(HALF, HALF)), picked[1][:, 0, HALF:], SUB)
-        for first in (0, CH):
-            cols = slice(first, first + CH)
-            nc.scalar.activation(v23[:, 1, cols], vec_t[3][:].indirect(listed(first, CH)), COPY)
-            nc.vector.tensor_tensor(
-                x23[:, 1, cols],
-                vec_t[3][:].indirect(listed(HALF + first, CH)),
-                picked[1][:, 1, HALF + first : HALF + first + CH],
-                SUB,
-            )
-        for first in (0, CH):
-            cols = slice(first, first + CH)
-            nc.vector.tensor_tensor(
-                xb[0][:, cols, 2:4],
-                v23[:, :, cols].rearrange("p t i -> p i t"),
-                picked[1][:, :, cols].rearrange("p t i -> p i t"),
-                SUB,
-            )
-            nc.scalar.activation(xb[1][:, cols, 2:4], x23[:, :, cols].rearrange("p t i -> p i t"), IDENT)
+        def round_x(x, places, c):
+            h, first = divmod(c * CH, HALF)
+            return xb[h][:, first : first + CH, places], x[:, :, c * CH : (c + 1) * CH].rearrange("p t i -> p i t")
+
+        for c in range(3):
+            nc.scalar.activation(*round_x(x01, slice(0, 2), c), IDENT)
+        nc.vector.tensor_copy(*round_x(x01, slice(0, 2), 3))
+        for c in range(4):
+            cols = slice(c * CH, (c + 1) * CH)
+            nc.vector.tensor_tensor(x23[:, 1, cols], vec_t[3][:].indirect(listed(c * CH, CH)), picked[1][:, 1, cols], SUB)
+        for c in (0, 1):
+            nc.scalar.activation(*round_x(x23, slice(2, 4), c), IDENT)
+        nc.vector.tensor_copy(*round_x(x23, slice(2, 4), 2))
+        nc.scalar.activation(*round_x(x23, slice(2, 4), 3), IDENT)
 
         def quantize_x(h):
             nc.vector.quantize_mx(
@@ -128,9 +119,8 @@ def tile_attend_pqremainder_pl_kernel(tc, vec, book, wo, bias, offs, offs2, out_
         quantize_wo(0, 1)
         quantize_wo(1, 1)
         nc.vector.tensor_copy(*round_wo(1, WO_SPLIT[1], WO_SPLIT[2]))
-        quantize_wo(2, 1)
-        quantize_wo(3, 1)
-        x_codes.append(sb.tile([P, HALF], U32, name="late_codes", tag="wb1", align_bytes=64))
+        quantize_wo(2, 2)
+        x_codes.append(sb.tile([P, HALF], U32, name="late_codes", tag="wo_slot", align_bytes=64))
         quantize_x(1)
 
         y = [sb.tile([P, PACK, HALF], F32, name="y%d" % h) for h in range(2)]
@@ -179,7 +169,7 @@ def tile_attend_pqremainder_pl_kernel(tc, vec, book, wo, bias, offs, offs2, out_
         def weave_views(h, first, count):
             chunk, inside = divmod(h * HALF + first, CH)
             if chunk not in yb:
-                yb[chunk] = sb.tile([P, CH, PACK], BF16, name="yb", tag="yb%d" % (0, 1, 0, 3)[chunk], align_bytes=64)
+                yb[chunk] = sb.tile([P, CH, PACK], BF16, name="yb", tag="yb%d" % chunk, align_bytes=64)
             dst = yb[chunk][:].rearrange("p (c i) j -> p c j i", i=4)
             src = y[h][:].rearrange("p j (c i) -> p c j i", i=4)
             return dst[:, inside // 4 : (inside + count) // 4, :, :], src[:, first // 4 : (first + count) // 4, :, :]
@@ -195,30 +185,29 @@ def tile_attend_pqremainder_pl_kernel(tc, vec, book, wo, bias, offs, offs2, out_
         def store_words(h):
             nc.sync.dma_start(words_v[:, h * HALF : (h + 1) * HALF], y_codes[h][:].bitcast(I32))
 
-        for j in range(2):
-            project(j, 0, 0, HALF, "bank%d" % j)
-            store_rows(0, j, 1, 0, HALF)
         for first in (0, CH):
-            project(2, 0, first, CH, "bank%d" % (2 + 2 * (first // CH)))
-            project_on_vector(3, 0, first, CH, "bank%d" % (3 + 2 * (first // CH)))
-        store_rows(0, 2, 1, 0, HALF)
-        store_rows(0, 3, 1, 0, HALF)
+            project(0, 0, first, CH, "bank%d" % (first // CH))
+            store_rows(0, 0, 1, first, CH)
+        project(1, 0, 0, HALF, "bank2")
+        store_rows(0, 1, 1, 0, HALF)
+        for first in (0, CH):
+            project_pair(0, first, "bank%d" % (3 + first // CH))
+        store_rows(0, 2, 2, 0, HALF)
         for first in (0, CH):
             nc.vector.tensor_copy(*weave_views(0, first, CH))
-        project(0, 1, 0, HALF, "bank6")
-        project(1, 1, 0, HALF, "bank7")
-        store_rows(1, 0, 2, 0, HALF)
-        project(2, 1, 0, CH, "bank0")
-        project(3, 1, 0, CH, "bank1")
         for first in (0, CH):
             quantize_y(0, first, CH)
-        store_words(0)
-        project_on_vector(2, 1, CH, CH, "bank4")
-        project(3, 1, CH, CH, "bank5")
+        project(0, 1, 0, HALF, "bank5")
+        project(1, 1, 0, HALF, "bank6")
+        store_rows(1, 0, 2, 0, HALF)
+        project(2, 1, 0, HALF, "bank7")
+        for first in (0, CH):
+            project(3, 1, first, CH, "bank%d" % (first // CH))
         store_rows(1, 2, 2, 0, HALF)
-        nc.vector.tensor_copy(*weave_views(1, 0, 56))
+        store_words(0)
+        nc.vector.tensor_copy(*weave_views(1, 0, 64))
         nc.vector.tensor_copy(*weave_views(1, CH, CH))
-        nc.scalar.activation(*weave_views(1, 56, 72), IDENT)
+        nc.scalar.activation(*weave_views(1, 64, 64), IDENT)
         for first in (0, CH):
             quantize_y(1, first, CH)
         store_words(1)

@@ -61,7 +61,8 @@ def tile_attend_pqremainder_pl_kernel(tc, vec, book, wo, bias, offs, offs2, out_
             nc.scalar.activation(picked[u][:, 1, :], book_t[odd][:].indirect(offs2_t[:]), COPY)
 
         x01 = sb.tile([P, 2, I], F32, name="x01")
-        x23 = sb.tile([P, 2, I], F32, name="x23")
+        v23 = sb.tile([P, 2, HALF], F32, name="v23")
+        x23 = sb.tile([P, 2, HALF], F32, name="x23")
         xb = [sb.tile([P, HALF, PACK], BF16, name="xb%d" % h, align_bytes=64) for h in range(2)]
         x_codes = [sb.tile([P, HALF], U32, name="lead_codes", align_bytes=64)]
         x_scales = [sb.tile([P, HALF], U8, name="x_scales%d" % h, align_bytes=64) for h in range(2)]
@@ -75,22 +76,30 @@ def tile_attend_pqremainder_pl_kernel(tc, vec, book, wo, bias, offs, offs2, out_
         nc.vector.tensor_tensor(x01[:, 0, :], vec01[:].indirect(offs_t[:]), picked[0][:, 0, :], SUB)
         nc.scalar.activation(v1[:], vec01[:, T:].indirect(offs_t[:]), COPY)
         nc.vector.tensor_tensor(x01[:, 1, :], v1[:], picked[0][:, 1, :], SUB)
-        nc.vector.tensor_tensor(x23[:, 0, :], vec_t[2][:].indirect(offs_t[:]), picked[1][:, 0, :], SUB)
+        for h in range(2):
+            cols = slice(h * HALF, (h + 1) * HALF)
+            nc.scalar.activation(xb[h][:, :, 0:2], x01[:, :, cols].rearrange("p t i -> p i t"), IDENT)
 
-        def round_x(x, places, c):
-            h, first = divmod(c * CH, HALF)
-            return xb[h][:, first : first + CH, places], x[:, :, c * CH : (c + 1) * CH].rearrange("p t i -> p i t")
-
-        for c in range(3):
-            nc.scalar.activation(*round_x(x01, slice(0, 2), c), IDENT)
-        nc.vector.tensor_copy(*round_x(x01, slice(0, 2), 3))
-        for c in range(4):
-            cols = slice(c * CH, (c + 1) * CH)
-            nc.vector.tensor_tensor(x23[:, 1, cols], vec_t[3][:].indirect(listed(c * CH, CH)), picked[1][:, 1, cols], SUB)
-        for c in (0, 1):
-            nc.scalar.activation(*round_x(x23, slice(2, 4), c), IDENT)
-        nc.vector.tensor_copy(*round_x(x23, slice(2, 4), 2))
-        nc.scalar.activation(*round_x(x23, slice(2, 4), 3), IDENT)
+        nc.vector.tensor_copy(v23[:, 0, :], vec_t[2][:].indirect(listed(0, HALF)))
+        nc.vector.tensor_tensor(x23[:, 0, :], vec_t[2][:].indirect(listed(HALF, HALF)), picked[1][:, 0, HALF:], SUB)
+        for first in (0, CH):
+            cols = slice(first, first + CH)
+            nc.scalar.activation(v23[:, 1, cols], vec_t[3][:].indirect(listed(first, CH)), COPY)
+            nc.vector.tensor_tensor(
+                x23[:, 1, cols],
+                vec_t[3][:].indirect(listed(HALF + first, CH)),
+                picked[1][:, 1, HALF + first : HALF + first + CH],
+                SUB,
+            )
+        for first in (0, CH):
+            cols = slice(first, first + CH)
+            nc.vector.tensor_tensor(
+                xb[0][:, cols, 2:4],
+                v23[:, :, cols].rearrange("p t i -> p i t"),
+                picked[1][:, :, cols].rearrange("p t i -> p i t"),
+                SUB,
+            )
+            nc.scalar.activation(xb[1][:, cols, 2:4], x23[:, :, cols].rearrange("p t i -> p i t"), IDENT)
 
         def quantize_x(h):
             nc.vector.quantize_mx(

@@ -21,7 +21,7 @@ P = 128
 PACK = 4
 CH = 128
 HALF = 256
-WO_SPLIT = (84, 36, 72)
+WO_SPLIT = (80, 28, 72)
 
 
 def tile_attend_pqremainder_pl_kernel(tc, vec, book, wo, bias, offs, offs2, out_0, out_1, out_2):
@@ -128,7 +128,8 @@ def tile_attend_pqremainder_pl_kernel(tc, vec, book, wo, bias, offs, offs2, out_
         quantize_wo(0, 1)
         quantize_wo(1, 1)
         nc.vector.tensor_copy(*round_wo(1, WO_SPLIT[1], WO_SPLIT[2]))
-        quantize_wo(2, 2)
+        quantize_wo(2, 1)
+        quantize_wo(3, 1)
         x_codes.append(sb.tile([P, HALF], U32, name="late_codes", tag="wo_slot", align_bytes=64))
         quantize_x(1)
 
@@ -199,19 +200,20 @@ def tile_attend_pqremainder_pl_kernel(tc, vec, book, wo, bias, offs, offs2, out_
             store_rows(0, 0, 1, first, CH)
         project(1, 0, 0, HALF, "bank2")
         store_rows(0, 1, 1, 0, HALF)
-        for first in (0, CH):
-            project_pair(0, first, "bank%d" % (3 + first // CH))
+        project_pair(0, 0, "bank3")
+        project_on_vector(2, 0, CH, CH, "bank4")
+        project(3, 0, CH, CH, "bank5")
         store_rows(0, 2, 2, 0, HALF)
         for first in (0, CH):
             nc.vector.tensor_copy(*weave_views(0, first, CH))
         for first in (0, CH):
             quantize_y(0, first, CH)
-        project(0, 1, 0, HALF, "bank5")
-        project(1, 1, 0, HALF, "bank6")
+        project(0, 1, 0, HALF, "bank6")
+        project(1, 1, 0, HALF, "bank7")
         store_rows(1, 0, 2, 0, HALF)
-        project(2, 1, 0, HALF, "bank7")
+        project(2, 1, 0, HALF, "bank0")
         for first in (0, CH):
-            project(3, 1, first, CH, "bank%d" % (first // CH))
+            project(3, 1, first, CH, "bank%d" % (1 + first // CH))
         store_rows(1, 2, 2, 0, HALF)
         store_words(0)
         nc.vector.tensor_copy(*weave_views(1, 0, 64))

@@ -216,9 +216,9 @@ def tile_attend_pqremainder_pl_kernel(tc, vec, book, wo, bias, offs, offs2, out_
             project(3, 1, first, CH, "bank%d" % (1 + first // CH))
         store_rows(1, 2, 2, 0, HALF)
         store_words(0)
-        nc.vector.tensor_copy(*weave_views(1, 0, 64))
+        nc.vector.tensor_copy(*weave_views(1, 0, 88))
         nc.vector.tensor_copy(*weave_views(1, CH, CH))
-        nc.scalar.activation(*weave_views(1, 64, 64), IDENT)
+        nc.scalar.activation(*weave_views(1, 88, 40), IDENT)
         for first in (0, CH):
             quantize_y(1, first, CH)
         store_words(1)

@@ -133,7 +133,8 @@ def tile_attend_pqremainder_pl_kernel(tc, vec, book, wo, bias, offs, offs2, out_
         x_codes.append(sb.tile([P, HALF], U32, name="late_codes", tag="wo_slot", align_bytes=64))
         quantize_x(1)
 
-        y = [sb.tile([P, PACK, HALF], F32, name="y%d" % h) for h in range(2)]
+        y_all = sb.tile([P, PACK, I], F32, name="y_all")
+        y = [y_all[:, :, h * HALF : (h + 1) * HALF] for h in range(2)]
         yb = {}
         y_codes = [sb.tile([P, HALF], U32, name="y_codes%d" % h, align_bytes=64) for h in range(2)]
         y_scales = sb.tile([P, I], U8, name="y_scales", align_bytes=64)
@@ -176,12 +177,16 @@ def tile_attend_pqremainder_pl_kernel(tc, vec, book, wo, bias, offs, offs2, out_
             lo = h * HALF + first
             nc.sync.dma_start(out0_v[:, j : j + rows, lo : lo + count], y[h][:, j : j + rows, first : first + count])
 
+        def store_run(j, h, halves):
+            run = slice(j * I + h * HALF, j * I + (h + halves) * HALF)
+            nc.sync.dma_start(out_0.rearrange("(p j) i -> p (j i)", j=PACK)[:, run], y_all[:].rearrange("p j i -> p (j i)")[:, run])
+
         def weave_views(h, first, count):
             chunk, inside = divmod(h * HALF + first, CH)
             if chunk not in yb:
                 yb[chunk] = sb.tile([P, CH, PACK], BF16, name="yb", tag="yb%d" % chunk, align_bytes=64)
             dst = yb[chunk][:].rearrange("p (c i) j -> p c j i", i=4)
-            src = y[h][:].rearrange("p j (c i) -> p c j i", i=4)
+            src = y[h].rearrange("p j (c i) -> p c j i", i=4)
             return dst[:, inside // 4 : (inside + count) // 4, :, :], src[:, first // 4 : (first + count) // 4, :, :]
 
         def quantize_y(h, first, count):
@@ -195,25 +200,25 @@ def tile_attend_pqremainder_pl_kernel(tc, vec, book, wo, bias, offs, offs2, out_
         def store_words(h):
             nc.sync.dma_start(words_v[:, h * HALF : (h + 1) * HALF], y_codes[h][:].bitcast(I32))
 
-        for first in (0, CH):
-            project(0, 0, first, CH, "bank%d" % (first // CH))
-            store_rows(0, 0, 1, first, CH)
+        project(0, 0, 0, HALF, "bank0")
+        store_rows(0, 0, 1, 0, HALF)
         project(1, 0, 0, HALF, "bank2")
         store_rows(0, 1, 1, 0, HALF)
         project_pair(0, 0, "bank3")
         project_on_vector(2, 0, CH, CH, "bank4")
         project(3, 0, CH, CH, "bank5")
-        store_rows(0, 2, 2, 0, HALF)
+        store_rows(0, 3, 1, 0, HALF)
         for first in (0, CH):
             nc.vector.tensor_copy(*weave_views(0, first, CH))
         for first in (0, CH):
             quantize_y(0, first, CH)
         project(0, 1, 0, HALF, "bank6")
+        store_rows(1, 0, 1, 0, HALF)
         project(1, 1, 0, HALF, "bank7")
-        store_rows(1, 0, 2, 0, HALF)
-        project(2, 1, 0, HALF, "bank0")
+        store_run(1, 1, 2)
+        project(2, 1, 0, HALF, "bank1")
         for first in (0, CH):
-            project(3, 1, first, CH, "bank%d" % (1 + first // CH))
+            project(3, 1, first, CH, "bank%d" % (2 * (first // CH)))
         store_rows(1, 2, 2, 0, HALF)
         store_words(0)
         nc.vector.tensor_copy(*weave_views(1, 0, 88))

@@ -21,7 +21,7 @@ P = 128
 PACK = 4
 CH = 128
 HALF = 256
-WO_SPLIT = (80, 28, 72)
+WO_SPLIT = (80, 36, 72)
 
 
 def tile_attend_pqremainder_pl_kernel(tc, vec, book, wo, bias, offs, offs2, out_0, out_1, out_2):
@@ -126,8 +126,8 @@ def tile_attend_pqremainder_pl_kernel(tc, vec, book, wo, bias, offs, offs2, out_
         nc.vector.tensor_copy(*round_wo(1, 0, WO_SPLIT[1]))
         nc.scalar.activation(*round_wo(1, WO_SPLIT[2], P), IDENT)
         quantize_wo(0, 1)
-        quantize_wo(1, 1)
         nc.vector.tensor_copy(*round_wo(1, WO_SPLIT[1], WO_SPLIT[2]))
+        quantize_wo(1, 1)
         quantize_wo(2, 1)
         quantize_wo(3, 1)
         x_codes.append(sb.tile([P, HALF], U32, name="late_codes", tag="wo_slot", align_bytes=64))

@@ -22,6 +22,7 @@ PACK = 4
 CH = 128
 HALF = 256
 WO_SPLIT = (80, 36, 72)
+SCALAR_WEAVE = 40
 
 
 def tile_attend_pqremainder_pl_kernel(tc, vec, book, wo, bias, offs, offs2, out_0, out_1, out_2):
@@ -61,18 +62,10 @@ def tile_attend_pqremainder_pl_kernel(tc, vec, book, wo, bias, offs, offs2, out_
             nc.scalar.activation(picked[u][:, 1, :], book_t[odd][:].indirect(offs2_t[:]), COPY)
 
         x01 = sb.tile([P, 2, I], F32, name="x01")
-        v23 = sb.tile([P, 2, HALF], F32, name="v23")
-        x23 = sb.tile([P, 2, HALF], F32, name="x23")
-        xb = [sb.tile([P, HALF, PACK], BF16, name="xb%d" % h, align_bytes=64) for h in range(2)]
-        x_codes = [sb.tile([P, HALF], U32, name="lead_codes", align_bytes=64)]
-        x_scales = [sb.tile([P, HALF], U8, name="x_scales%d" % h, align_bytes=64) for h in range(2)]
-        wb = [sb.tile([P, 2, P, PACK], BF16, name="wb%d" % u, tag="wb%d" % u, align_bytes=64) for u in range(2)]
-        wq_codes = sb.tile([P, PACK * P], U32, name="wq_codes", align_bytes=64)
-        wq_scales = sb.tile([P, PACK * P], U8, name="wq_scales", align_bytes=64)
-        w_codes = [wq_codes[:, j * P : (j + 1) * P] for j in range(PACK)]
-        w_scales = [wq_scales[:, j * P : (j + 1) * P] for j in range(PACK)]
-
         v1 = sb.tile([P, I], F32, name="v1")
+        xb = [sb.tile([P, HALF, PACK], BF16, name="xb%d" % h, align_bytes=64) for h in range(2)]
+        x_codes = [sb.tile([P, HALF], U32, name="x_codes0", align_bytes=64)]
+        x_scales = [sb.tile([P, HALF], U8, name="x_scales%d" % h, align_bytes=64) for h in range(2)]
         nc.vector.tensor_tensor(x01[:, 0, :], vec01[:].indirect(offs_t[:]), picked[0][:, 0, :], SUB)
         nc.scalar.activation(v1[:], vec01[:, T:].indirect(offs_t[:]), COPY)
         nc.vector.tensor_tensor(x01[:, 1, :], v1[:], picked[0][:, 1, :], SUB)
@@ -80,8 +73,16 @@ def tile_attend_pqremainder_pl_kernel(tc, vec, book, wo, bias, offs, offs2, out_
             cols = slice(h * HALF, (h + 1) * HALF)
             nc.scalar.activation(xb[h][:, :, 0:2], x01[:, :, cols].rearrange("p t i -> p i t"), IDENT)
 
+        v23 = sb.tile([P, 2, HALF], F32, name="v23")
+        x23 = sb.tile([P, 2, HALF], F32, name="x23")
         nc.vector.tensor_copy(v23[:, 0, :], vec_t[2][:].indirect(listed(0, HALF)))
         nc.vector.tensor_tensor(x23[:, 0, :], vec_t[2][:].indirect(listed(HALF, HALF)), picked[1][:, 0, HALF:], SUB)
+
+        def quantize_x(h):
+            nc.vector.quantize_mx(
+                out=x_codes[h][:].bitcast(FP8X4), scales=x_scales[h][:], in_=xb[h][:].rearrange("p c t -> p (c t)")
+            )
+
         for first in (0, CH):
             cols = slice(first, first + CH)
             nc.scalar.activation(v23[:, 1, cols], vec_t[3][:].indirect(listed(first, CH)), COPY)
@@ -100,132 +101,107 @@ def tile_attend_pqremainder_pl_kernel(tc, vec, book, wo, bias, offs, offs2, out_
                 SUB,
             )
             nc.scalar.activation(xb[1][:, cols, 2:4], x23[:, :, cols].rearrange("p t i -> p i t"), IDENT)
-
-        def quantize_x(h):
-            nc.vector.quantize_mx(
-                out=x_codes[h][:].bitcast(FP8X4), scales=x_scales[h][:], in_=xb[h][:].rearrange("p c t -> p (c t)")
-            )
-
         quantize_x(0)
 
-        def quantize_wo(first, count):
-            u, e = divmod(first, 2)
+        wb = [sb.tile([P, 2, P, PACK], BF16, name="wb%d" % u, align_bytes=64) for u in range(2)]
+        w_codes = sb.tile([P, PACK * P], U32, name="w_codes", align_bytes=64)
+        w_scales = sb.tile([P, PACK * P], U8, name="w_scales", align_bytes=64)
+
+        def wo_views(u, lo, hi):
+            dst = wb[u][:].rearrange("p j m t -> p m t j")
+            src = wo_raw[:].rearrange("p t (m j) -> p m t j", j=PACK)[:, :, :, 2 * u : 2 * u + 2]
+            return dst[:, lo:hi], src[:, lo:hi]
+
+        def quantize_wo(j):
+            cols = slice(j * P, (j + 1) * P)
             nc.vector.quantize_mx(
-                out=wq_codes[:, first * P : (first + count) * P].bitcast(FP8X4),
-                scales=wq_scales[:, first * P : (first + count) * P],
-                in_=wb[u][:, e : e + count, :, :].rearrange("p e m t -> p (e m t)"),
+                out=w_codes[:, cols].bitcast(FP8X4),
+                scales=w_scales[:, cols],
+                in_=wb[j // 2][:, j % 2].rearrange("p m t -> p (m t)"),
             )
 
-        wo_v = wo_raw[:].rearrange("p t (m j) -> p m t j", j=PACK)
-
-        def round_wo(u, lo, hi):
-            return wb[u][:].rearrange("p j m t -> p m t j")[:, lo:hi, :, :], wo_v[:, lo:hi, :, 2 * u : 2 * u + 2]
-
-        nc.vector.tensor_copy(*round_wo(0, 0, WO_SPLIT[0]))
-        nc.scalar.activation(*round_wo(0, WO_SPLIT[0], P), IDENT)
-        nc.vector.tensor_copy(*round_wo(1, 0, WO_SPLIT[1]))
-        nc.scalar.activation(*round_wo(1, WO_SPLIT[2], P), IDENT)
-        quantize_wo(0, 1)
-        nc.vector.tensor_copy(*round_wo(1, WO_SPLIT[1], WO_SPLIT[2]))
-        quantize_wo(1, 1)
-        quantize_wo(2, 1)
-        quantize_wo(3, 1)
-        x_codes.append(sb.tile([P, HALF], U32, name="late_codes", tag="wo_slot", align_bytes=64))
+        nc.vector.tensor_copy(*wo_views(0, 0, WO_SPLIT[0]))
+        nc.scalar.activation(*wo_views(0, WO_SPLIT[0], P), IDENT)
+        nc.vector.tensor_copy(*wo_views(1, 0, WO_SPLIT[1]))
+        nc.scalar.activation(*wo_views(1, WO_SPLIT[2], P), IDENT)
+        quantize_wo(0)
+        nc.vector.tensor_copy(*wo_views(1, WO_SPLIT[1], WO_SPLIT[2]))
+        for j in (1, 2, 3):
+            quantize_wo(j)
+        x_codes.append(sb.tile([P, HALF], U32, name="x_codes1", tag="wo_slot", align_bytes=64))
         quantize_x(1)
 
-        y_all = sb.tile([P, PACK, I], F32, name="y_all")
-        y = [y_all[:, :, h * HALF : (h + 1) * HALF] for h in range(2)]
-        yb = {}
+        y = sb.tile([P, PACK, I], F32, name="y")
+        yb = [sb.tile([P, CH, PACK], BF16, name="yb%d" % c, align_bytes=64) for c in range(I // CH)]
         y_codes = [sb.tile([P, HALF], U32, name="y_codes%d" % h, align_bytes=64) for h in range(2)]
         y_scales = sb.tile([P, I], U8, name="y_scales", align_bytes=64)
         out0_v = out_0.rearrange("(p j) i -> p j i", j=PACK)
         words_v = out_1[0].rearrange("l c r -> l (c r)").bitcast(I32)
         scales_v = out_2[0].bitcast(I32)
 
-        def multiply(acc, j, h, first, count):
+        def project(j, first, count, bank, on_vector=False):
+            h, inside = divmod(first, HALF)
+            acc = ps.tile([P, count], F32, name="acc", tag=bank)
             nc.tensor.matmul_mx(
-                out=acc,
-                lhsT=w_codes[j].bitcast(FP8X4),
-                lhsT_scale=w_scales[j],
-                rhs=x_codes[h][:, first : first + count].bitcast(FP8X4),
-                rhs_scale=x_scales[h][:, first : first + count],
+                out=acc[:],
+                lhsT=w_codes[:, j * P : (j + 1) * P].bitcast(FP8X4),
+                lhsT_scale=w_scales[:, j * P : (j + 1) * P],
+                rhs=x_codes[h][:, inside : inside + count].bitcast(FP8X4),
+                rhs_scale=x_scales[h][:, inside : inside + count],
                 start=True,
                 stop=True,
             )
+            dst = y[:, j, first : first + count]
+            if on_vector:
+                nc.vector.tensor_tensor(dst, acc[:], bias_t[:, j : j + 1].to_broadcast([P, count]), ADD)
+            else:
+                nc.scalar.activation(dst, acc[:], IDENT, bias=bias_t[:, j : j + 1])
 
-        def project(j, h, first, count, bank):
-            acc = ps.tile([P, count], F32, name="acc", tag=bank)
-            multiply(acc[:], j, h, first, count)
-            nc.scalar.activation(y[h][:, j, first : first + count], acc[:], IDENT, bias=bias_t[:, j : j + 1])
+        def store_rows(j, rows, h):
+            cols = slice(h * HALF, (h + 1) * HALF)
+            nc.sync.dma_start(out0_v[:, j : j + rows, cols], y[:, j : j + rows, cols])
 
-        def project_pair(h, first, bank):
-            acc = ps.tile([P, 2, CH], F32, name="pair", tag=bank)
-            for e in range(2):
-                multiply(acc[:, e, :], 2 + e, h, first, CH)
-            nc.vector.tensor_tensor(
-                y[h][:, 2:4, first : first + CH], acc[:], bias_t[:, 2:4].unsqueeze(2).to_broadcast([P, 2, CH]), ADD
-            )
+        def weave_views(c, lo, hi):
+            dst = yb[c][:].rearrange("p (c i) j -> p c j i", i=4)
+            src = y[:, :, c * CH : (c + 1) * CH].rearrange("p j (c i) -> p c j i", i=4)
+            return dst[:, lo // 4 : hi // 4], src[:, lo // 4 : hi // 4]
 
-        def project_on_vector(j, h, first, count, bank):
-            acc = ps.tile([P, count], F32, name="acc", tag=bank)
-            multiply(acc[:], j, h, first, count)
-            nc.vector.tensor_tensor(
-                y[h][:, j, first : first + count], acc[:], bias_t[:, j : j + 1].to_broadcast([P, count]), ADD
-            )
-
-        def store_rows(h, j, rows, first, count):
-            lo = h * HALF + first
-            nc.sync.dma_start(out0_v[:, j : j + rows, lo : lo + count], y[h][:, j : j + rows, first : first + count])
-
-        def store_run(j, h, halves):
-            run = slice(j * I + h * HALF, j * I + (h + halves) * HALF)
-            nc.sync.dma_start(out_0.rearrange("(p j) i -> p (j i)", j=PACK)[:, run], y_all[:].rearrange("p j i -> p (j i)")[:, run])
-
-        def weave_views(h, first, count):
-            chunk, inside = divmod(h * HALF + first, CH)
-            if chunk not in yb:
-                yb[chunk] = sb.tile([P, CH, PACK], BF16, name="yb", tag="yb%d" % chunk, align_bytes=64)
-            dst = yb[chunk][:].rearrange("p (c i) j -> p c j i", i=4)
-            src = y[h].rearrange("p j (c i) -> p c j i", i=4)
-            return dst[:, inside // 4 : (inside + count) // 4, :, :], src[:, first // 4 : (first + count) // 4, :, :]
-
-        def quantize_y(h, first, count):
-            lo = h * HALF + first
+        def quantize_y(c):
+            h, inside = divmod(c * CH, HALF)
             nc.vector.quantize_mx(
-                out=y_codes[h][:, first : first + count].bitcast(FP8X4),
-                scales=y_scales[:, lo : lo + count],
-                in_=yb[lo // CH][:].rearrange("p c t -> p (c t)"),
+                out=y_codes[h][:, inside : inside + CH].bitcast(FP8X4),
+                scales=y_scales[:, c * CH : (c + 1) * CH],
+                in_=yb[c][:].rearrange("p c t -> p (c t)"),
             )
 
         def store_words(h):
             nc.sync.dma_start(words_v[:, h * HALF : (h + 1) * HALF], y_codes[h][:].bitcast(I32))
 
-        project(0, 0, 0, HALF, "bank0")
-        store_rows(0, 0, 1, 0, HALF)
-        project(1, 0, 0, HALF, "bank2")
-        store_rows(0, 1, 1, 0, HALF)
-        project_pair(0, 0, "bank3")
-        project_on_vector(2, 0, CH, CH, "bank4")
-        project(3, 0, CH, CH, "bank5")
-        store_rows(0, 3, 1, 0, HALF)
-        for first in (0, CH):
-            nc.vector.tensor_copy(*weave_views(0, first, CH))
-        for first in (0, CH):
-            quantize_y(0, first, CH)
-        project(0, 1, 0, HALF, "bank6")
-        store_rows(1, 0, 1, 0, HALF)
-        project(1, 1, 0, HALF, "bank7")
-        store_run(1, 1, 2)
-        project(2, 1, 0, HALF, "bank1")
-        for first in (0, CH):
-            project(3, 1, first, CH, "bank%d" % (2 * (first // CH)))
-        store_rows(1, 2, 2, 0, HALF)
+        for j in (0, 1):
+            project(j, 0, HALF, "bank%d" % j)
+            store_rows(j, 1, 0)
+        project(2, 0, HALF, "bank2", on_vector=True)
+        store_rows(2, 1, 0)
+        project(3, 0, CH, "bank3")
+        project(3, CH, CH, "bank4", on_vector=True)
+        store_rows(3, 1, 0)
+        for c in (0, 1):
+            nc.vector.tensor_copy(*weave_views(c, 0, CH))
+        for c in (0, 1):
+            quantize_y(c)
+        for j in (0, 1):
+            project(j, HALF, HALF, "bank%d" % (5 + j))
+        store_rows(0, 2, 1)
+        project(2, HALF, HALF, "bank7")
+        project(3, HALF, CH, "bank0")
+        project(3, HALF + CH, CH, "bank1")
         store_words(0)
-        nc.vector.tensor_copy(*weave_views(1, 0, 88))
-        nc.vector.tensor_copy(*weave_views(1, CH, CH))
-        nc.scalar.activation(*weave_views(1, 88, 40), IDENT)
-        for first in (0, CH):
-            quantize_y(1, first, CH)
+        store_rows(2, 2, 1)
+        nc.vector.tensor_copy(*weave_views(2, 0, CH - SCALAR_WEAVE))
+        nc.vector.tensor_copy(*weave_views(3, 0, CH))
+        nc.scalar.activation(*weave_views(2, CH - SCALAR_WEAVE, CH), IDENT)
+        for c in (2, 3):
+            quantize_y(c)
         store_words(1)
         for q in range(4):
             nc.scalar.dma_start(scales_v[4 * q : 4 * q + 4, :], y_scales[32 * q : 32 * q + 4, :].bitcast(I32))

@@ -103,6 +103,19 @@ def tile_attend_pqremainder_pl_kernel(tc, vec, book, wo, bias, offs, offs2, out_
             nc.scalar.activation(xb[1][:, cols, 2:4], x23[:, :, cols].rearrange("p t i -> p i t"), IDENT)
         quantize_x(0)
 
+        for bank in ("bank6", "bank7"):
+            idle = ps.tile([P, 3, CH], F32, name="idle", tag=bank)
+            for e in range(3):
+                nc.tensor.matmul_mx(
+                    out=idle[0:32, e, :],
+                    lhsT=x_codes[0][:, 0:32].bitcast(FP8X4),
+                    lhsT_scale=x_scales[0][:, 0:32],
+                    rhs=x_codes[0][:, 0:CH].bitcast(FP8X4),
+                    rhs_scale=x_scales[0][:, 0:CH],
+                    start=True,
+                    stop=True,
+                )
+
         wb = [sb.tile([P, 2, P, PACK], BF16, name="wb%d" % u, align_bytes=64) for u in range(2)]
         w_codes = sb.tile([P, PACK * P], U32, name="w_codes", align_bytes=64)
         w_scales = sb.tile([P, PACK * P], U8, name="w_scales", align_bytes=64)

@@ -34,11 +34,11 @@ def tile_attend_pqremainder_pl_kernel(tc, vec, book, wo, bias, offs, offs2, out_
         offs_t = sb.tile([P, I // 16], U16, name="offs_t")
         offs2_t = sb.tile([P, I // 16], U16, name="offs2_t")
         bias_t = sb.tile([P, PACK], F32, name="bias_t")
-        book_raw = sb.tile([P, PACK * C], F32, name="book_raw")
+        book_raw = sb.tile([P, PACK * C], F32, name="book_raw", align_bytes=256)
         book_t = [sb.tile([P, C], F32, name="book%d" % t) for t in range(PACK)]
-        vec01 = sb.tile([P, 2 * T], F32, name="vec01")
-        vec_t = {t: sb.tile([P, T], F32, name="vec%d" % t) for t in (2, 3)}
-        wo_raw = sb.tile([P, PACK, F], F32, name="wo_raw", tag="wo_slot", align_bytes=64)
+        vec01 = sb.tile([P, 2 * T], F32, name="vec01", align_bytes=256)
+        vec_t = {t: sb.tile([P, T], F32, name="vec%d" % t, align_bytes=256) for t in (2, 3)}
+        wo_raw = sb.tile([P, PACK, F], F32, name="wo_raw", tag="wo_slot", align_bytes=256)
 
         vec_v = vec.rearrange("(p t) c -> p t c", t=PACK)
         nc.sync.dma_start(book_raw[:], book.rearrange("(p t) c -> p (t c)", t=PACK))
@@ -141,13 +141,13 @@ def tile_attend_pqremainder_pl_kernel(tc, vec, book, wo, bias, offs, offs2, out_
         nc.vector.tensor_copy(*wo_views(1, WO_SPLIT[1], WO_SPLIT[2]))
         for j in (1, 2, 3):
             quantize_wo(j)
-        x_codes.append(sb.tile([P, HALF], U32, name="x_codes1", tag="wo_slot", align_bytes=64))
+        x_codes.append(sb.tile([P, HALF], U32, name="x_codes1", tag="wo_slot", align_bytes=256))
         quantize_x(1)
 
-        y = sb.tile([P, PACK, I], F32, name="y")
+        y = sb.tile([P, PACK, I], F32, name="y", align_bytes=256)
         yb = [sb.tile([P, CH, PACK], BF16, name="yb%d" % c, align_bytes=64) for c in range(I // CH)]
-        y_codes = [sb.tile([P, HALF], U32, name="y_codes%d" % h, align_bytes=64) for h in range(2)]
-        y_scales = sb.tile([P, I], U8, name="y_scales", align_bytes=64)
+        y_codes = [sb.tile([P, HALF], U32, name="y_codes%d" % h, align_bytes=256) for h in range(2)]
+        y_scales = sb.tile([P, I], U8, name="y_scales", align_bytes=256)
         out0_v = out_0.rearrange("(p j) i -> p j i", j=PACK)
         words_v = out_1[0].rearrange("l c r -> l (c r)").bitcast(I32)
         scales_v = out_2[0].bitcast(I32)

@@ -146,7 +146,7 @@ def tile_attend_pqremainder_pl_kernel(tc, vec, book, wo, bias, offs, offs2, out_
 
         y = sb.tile([P, PACK, I], F32, name="y", align_bytes=256)
         yb = [sb.tile([P, CH, PACK], BF16, name="yb%d" % c, align_bytes=64) for c in range(I // CH)]
-        y_codes = [sb.tile([P, HALF], U32, name="y_codes%d" % h, align_bytes=256) for h in range(2)]
+        y_codes = sb.tile([P, I], U32, name="y_codes", align_bytes=256)
         y_scales = sb.tile([P, I], U8, name="y_scales", align_bytes=256)
         out0_v = out_0.rearrange("(p j) i -> p j i", j=PACK)
         words_v = out_1[0].rearrange("l c r -> l (c r)").bitcast(I32)
@@ -180,15 +180,14 @@ def tile_attend_pqremainder_pl_kernel(tc, vec, book, wo, bias, offs, offs2, out_
             return dst[:, lo // 4 : hi // 4], src[:, lo // 4 : hi // 4]
 
         def quantize_y(c):
-            h, inside = divmod(c * CH, HALF)
             nc.vector.quantize_mx(
-                out=y_codes[h][:, inside : inside + CH].bitcast(FP8X4),
+                out=y_codes[:, c * CH : (c + 1) * CH].bitcast(FP8X4),
                 scales=y_scales[:, c * CH : (c + 1) * CH],
                 in_=yb[c][:].rearrange("p c t -> p (c t)"),
             )
 
-        def store_words(h):
-            nc.sync.dma_start(words_v[:, h * HALF : (h + 1) * HALF], y_codes[h][:].bitcast(I32))
+        def store_words(lo, hi):
+            nc.sync.dma_start(words_v[:, lo:hi], y_codes[:, lo:hi].bitcast(I32))
 
         for j in (0, 1):
             project(j, 0, HALF, "bank%d" % j)
@@ -208,13 +207,14 @@ def tile_attend_pqremainder_pl_kernel(tc, vec, book, wo, bias, offs, offs2, out_
         project(2, HALF, HALF, "bank7")
         project(3, HALF, CH, "bank0")
         project(3, HALF + CH, CH, "bank1")
-        store_words(0)
         store_rows(2, 2, 1)
         nc.vector.tensor_copy(*weave_views(2, 0, CH - SCALAR_WEAVE))
         nc.vector.tensor_copy(*weave_views(3, 0, CH))
         nc.scalar.activation(*weave_views(2, CH - SCALAR_WEAVE, CH), IDENT)
-        for c in (2, 3):
-            quantize_y(c)
-        store_words(1)
+        quantize_y(2)
+        store_words(0, 3 * CH)
+        quantize_y(3)
+        store_words(3 * CH, I)
         for q in range(4):
-            nc.scalar.dma_start(scales_v[4 * q : 4 * q + 4, :], y_scales[32 * q : 32 * q + 4, :].bitcast(I32))
+            queue = nc.scalar if q < 2 else nc.sync
+            queue.dma_start(scales_v[4 * q : 4 * q + 4, :], y_scales[32 * q : 32 * q + 4, :].bitcast(I32))

@@ -146,7 +146,7 @@ def tile_attend_pqremainder_pl_kernel(tc, vec, book, wo, bias, offs, offs2, out_
 
         y = sb.tile([P, PACK, I], F32, name="y", align_bytes=256)
         yb = [sb.tile([P, CH, PACK], BF16, name="yb%d" % c, align_bytes=64) for c in range(I // CH)]
-        y_codes = sb.tile([P, I], U32, name="y_codes", align_bytes=256)
+        y_codes = [sb.tile([P, HALF], U32, name="y_codes%d" % h, align_bytes=256) for h in range(2)]
         y_scales = sb.tile([P, I], U8, name="y_scales", align_bytes=256)
         out0_v = out_0.rearrange("(p j) i -> p j i", j=PACK)
         words_v = out_1[0].rearrange("l c r -> l (c r)").bitcast(I32)
@@ -180,14 +180,15 @@ def tile_attend_pqremainder_pl_kernel(tc, vec, book, wo, bias, offs, offs2, out_
             return dst[:, lo // 4 : hi // 4], src[:, lo // 4 : hi // 4]
 
         def quantize_y(c):
+            h, inside = divmod(c * CH, HALF)
             nc.vector.quantize_mx(
-                out=y_codes[:, c * CH : (c + 1) * CH].bitcast(FP8X4),
+                out=y_codes[h][:, inside : inside + CH].bitcast(FP8X4),
                 scales=y_scales[:, c * CH : (c + 1) * CH],
                 in_=yb[c][:].rearrange("p c t -> p (c t)"),
             )
 
-        def store_words(lo, hi):
-            nc.sync.dma_start(words_v[:, lo:hi], y_codes[:, lo:hi].bitcast(I32))
+        def store_words(h):
+            nc.sync.dma_start(words_v[:, h * HALF : (h + 1) * HALF], y_codes[h][:].bitcast(I32))
 
         for j in (0, 1):
             project(j, 0, HALF, "bank%d" % j)
@@ -207,14 +208,14 @@ def tile_attend_pqremainder_pl_kernel(tc, vec, book, wo, bias, offs, offs2, out_
         project(2, HALF, HALF, "bank7")
         project(3, HALF, CH, "bank0")
         project(3, HALF + CH, CH, "bank1")
+        store_words(0)
         store_rows(2, 2, 1)
         nc.vector.tensor_copy(*weave_views(2, 0, CH - SCALAR_WEAVE))
         nc.vector.tensor_copy(*weave_views(3, 0, CH))
         nc.scalar.activation(*weave_views(2, CH - SCALAR_WEAVE, CH), IDENT)
-        quantize_y(2)
-        store_words(0, 3 * CH)
-        quantize_y(3)
-        store_words(3 * CH, I)
+        for c in (2, 3):
+            quantize_y(c)
+        store_words(1)
         for q in range(4):
             queue = nc.scalar if q < 2 else nc.sync
             queue.dma_start(scales_v[4 * q : 4 * q + 4, :], y_scales[32 * q : 32 * q + 4, :].bitcast(I32))

from contextlib import ExitStack

import concourse.mybir as mybir

D, T, I, C, F = 512, 2048, 512, 1024, 512
FLOPS = 2 * D * F * I

F32 = mybir.dt.float32
BF16 = mybir.dt.bfloat16
I32 = mybir.dt.int32
U32 = mybir.dt.uint32
U16 = mybir.dt.uint16
U8 = mybir.dt.uint8
FP8X4 = mybir.dt.float8_e4m3fn_x4
SUB = mybir.AluOpType.subtract
ADD = mybir.AluOpType.add
IDENT = mybir.ActivationFunctionType.Identity
COPY = mybir.ActivationFunctionType.Copy

P = 128
PACK = 4
CH = 128
HALF = 256
WO_SPLIT = (80, 36, 72)
SCALAR_WEAVE = 40


def tile_attend_pqremainder_pl_kernel(tc, vec, book, wo, bias, offs, offs2, out_0, out_1, out_2):
    nc = tc.nc
    with ExitStack() as ctx:
        sb = ctx.enter_context(tc.tile_pool(name="sb", bufs=1))
        ps = ctx.enter_context(tc.psum_pool(name="ps", bufs=1))

        offs_t = sb.tile([P, I // 16], U16, name="offs_t")
        offs2_t = sb.tile([P, I // 16], U16, name="offs2_t")
        bias_t = sb.tile([P, PACK], F32, name="bias_t")
        book_raw = sb.tile([P, PACK * C], F32, name="book_raw", align_bytes=256)
        book_t = [sb.tile([P, C], F32, name="book%d" % t) for t in range(PACK)]
        vec01 = sb.tile([P, 2 * T], F32, name="vec01", align_bytes=256)
        vec_t = {t: sb.tile([P, T], F32, name="vec%d" % t, align_bytes=256) for t in (2, 3)}
        wo_raw = sb.tile([P, PACK, F], F32, name="wo_raw", tag="wo_slot", align_bytes=256)

        vec_v = vec.rearrange("(p t) c -> p t c", t=PACK)
        nc.sync.dma_start(book_raw[:], book.rearrange("(p t) c -> p (t c)", t=PACK))
        nc.sync.dma_start(offs2_t[:], offs2)
        nc.sync.dma_start(offs_t[:], offs)
        nc.sync.dma_start(vec01[:], vec.rearrange("(p u e) c -> p u (e c)", u=2, e=2)[:, 0, :])
        for t in (2, 3):
            nc.sync.dma_start(vec_t[t][:], vec_v[:, t, :])
        nc.sync.dma_start(wo_raw[:], wo.rearrange("(p t) f -> p t f", t=PACK))
        nc.sync.dma_start(bias_t[:], bias.rearrange("(p j) o -> p (j o)", j=PACK))

        def listed(first, count):
            return offs_t[:, first // 16 : (first + count) // 16]

        picked = [sb.tile([P, 2, I], F32, name="picked%d" % u) for u in range(2)]
        for u in range(2):
            even, odd = 2 * u, 2 * u + 1
            nc.vector.tensor_copy(book_t[even][:], book_raw[:, even * C : (even + 1) * C])
            nc.vector.tensor_copy(picked[u][:, 0, :], book_t[even][:].indirect(offs2_t[:]))
            nc.scalar.activation(book_t[odd][:], book_raw[:, odd * C : (odd + 1) * C], IDENT)
            nc.scalar.activation(picked[u][:, 1, :], book_t[odd][:].indirect(offs2_t[:]), COPY)

        x01 = sb.tile([P, 2, I], F32, name="x01")
        v1 = sb.tile([P, I], F32, name="v1")
        xb = [sb.tile([P, HALF, PACK], BF16, name="xb%d" % h, align_bytes=64) for h in range(2)]
        x_codes = [sb.tile([P, HALF], U32, name="x_codes0", align_bytes=64)]
        x_scales = [sb.tile([P, HALF], U8, name="x_scales%d" % h, align_bytes=64) for h in range(2)]
        nc.vector.tensor_tensor(x01[:, 0, :], vec01[:].indirect(offs_t[:]), picked[0][:, 0, :], SUB)
        nc.scalar.activation(v1[:], vec01[:, T:].indirect(offs_t[:]), COPY)
        nc.vector.tensor_tensor(x01[:, 1, :], v1[:], picked[0][:, 1, :], SUB)
        for h in range(2):
            cols = slice(h * HALF, (h + 1) * HALF)
            nc.scalar.activation(xb[h][:, :, 0:2], x01[:, :, cols].rearrange("p t i -> p i t"), IDENT)

        v23 = sb.tile([P, 2, HALF], F32, name="v23")
        x23 = sb.tile([P, 2, HALF], F32, name="x23")
        nc.vector.tensor_copy(v23[:, 0, :], vec_t[2][:].indirect(listed(0, HALF)))
        nc.vector.tensor_tensor(x23[:, 0, :], vec_t[2][:].indirect(listed(HALF, HALF)), picked[1][:, 0, HALF:], SUB)

        def quantize_x(h):
            nc.vector.quantize_mx(
                out=x_codes[h][:].bitcast(FP8X4), scales=x_scales[h][:], in_=xb[h][:].rearrange("p c t -> p (c t)")
            )

        for first in (0, CH):
            cols = slice(first, first + CH)
            nc.scalar.activation(v23[:, 1, cols], vec_t[3][:].indirect(listed(first, CH)), COPY)
            nc.vector.tensor_tensor(
                x23[:, 1, cols],
                vec_t[3][:].indirect(listed(HALF + first, CH)),
                picked[1][:, 1, HALF + first : HALF + first + CH],
                SUB,
            )
        for first in (0, CH):
            cols = slice(first, first + CH)
            nc.vector.tensor_tensor(
                xb[0][:, cols, 2:4],
                v23[:, :, cols].rearrange("p t i -> p i t"),
                picked[1][:, :, cols].rearrange("p t i -> p i t"),
                SUB,
            )
            nc.scalar.activation(xb[1][:, cols, 2:4], x23[:, :, cols].rearrange("p t i -> p i t"), IDENT)
        quantize_x(0)

        for bank in ("bank6", "bank7"):
            idle = ps.tile([P, 3, CH], F32, name="idle", tag=bank)
            for e in range(3):
                nc.tensor.matmul_mx(
                    out=idle[0:32, e, :],
                    lhsT=x_codes[0][:, 0:32].bitcast(FP8X4),
                    lhsT_scale=x_scales[0][:, 0:32],
                    rhs=x_codes[0][:, 0:CH].bitcast(FP8X4),
                    rhs_scale=x_scales[0][:, 0:CH],
                    start=True,
                    stop=True,
                )

        wb = [sb.tile([P, 2, P, PACK], BF16, name="wb%d" % u, align_bytes=64) for u in range(2)]
        w_codes = sb.tile([P, PACK * P], U32, name="w_codes", align_bytes=64)
        w_scales = sb.tile([P, PACK * P], U8, name="w_scales", align_bytes=64)

        def wo_views(u, lo, hi):
            dst = wb[u][:].rearrange("p j m t -> p m t j")
            src = wo_raw[:].rearrange("p t (m j) -> p m t j", j=PACK)[:, :, :, 2 * u : 2 * u + 2]
            return dst[:, lo:hi], src[:, lo:hi]

        def quantize_wo(j):
            cols = slice(j * P, (j + 1) * P)
            nc.vector.quantize_mx(
                out=w_codes[:, cols].bitcast(FP8X4),
                scales=w_scales[:, cols],
                in_=wb[j // 2][:, j % 2].rearrange("p m t -> p (m t)"),
            )

        nc.vector.tensor_copy(*wo_views(0, 0, WO_SPLIT[0]))
        nc.scalar.activation(*wo_views(0, WO_SPLIT[0], P), IDENT)
        nc.vector.tensor_copy(*wo_views(1, 0, WO_SPLIT[1]))
        nc.scalar.activation(*wo_views(1, WO_SPLIT[2], P), IDENT)
        quantize_wo(0)
        nc.vector.tensor_copy(*wo_views(1, WO_SPLIT[1], WO_SPLIT[2]))
        for j in (1, 2, 3):
            quantize_wo(j)
        x_codes.append(sb.tile([P, HALF], U32, name="x_codes1", tag="wo_slot", align_bytes=256))
        quantize_x(1)

        y = sb.tile([P, PACK, I], F32, name="y", align_bytes=256)
        yb = [sb.tile([P, CH, PACK], BF16, name="yb%d" % c, align_bytes=64) for c in range(I // CH)]
        y_codes = [sb.tile([P, HALF], U32, name="y_codes%d" % h, align_bytes=256) for h in range(2)]
        y_scales = sb.tile([P, I], U8, name="y_scales", align_bytes=256)
        out0_v = out_0.rearrange("(p j) i -> p j i", j=PACK)
        words_v = out_1[0].rearrange("l c r -> l (c r)").bitcast(I32)
        scales_v = out_2[0].bitcast(I32)

        def project(j, first, count, bank, on_vector=False):
            h, inside = divmod(first, HALF)
            acc = ps.tile([P, count], F32, name="acc", tag=bank)
            nc.tensor.matmul_mx(
                out=acc[:],
                lhsT=w_codes[:, j * P : (j + 1) * P].bitcast(FP8X4),
                lhsT_scale=w_scales[:, j * P : (j + 1) * P],
                rhs=x_codes[h][:, inside : inside + count].bitcast(FP8X4),
                rhs_scale=x_scales[h][:, inside : inside + count],
                start=True,
                stop=True,
            )
            dst = y[:, j, first : first + count]
            if on_vector:
                nc.vector.tensor_tensor(dst, acc[:], bias_t[:, j : j + 1].to_broadcast([P, count]), ADD)
            else:
                nc.scalar.activation(dst, acc[:], IDENT, bias=bias_t[:, j : j + 1])

        def store_rows(j, rows, h):
            cols = slice(h * HALF, (h + 1) * HALF)
            nc.sync.dma_start(out0_v[:, j : j + rows, cols], y[:, j : j + rows, cols])

        def weave_views(c, lo, hi):
            dst = yb[c][:].rearrange("p (c i) j -> p c j i", i=4)
            src = y[:, :, c * CH : (c + 1) * CH].rearrange("p j (c i) -> p c j i", i=4)
            return dst[:, lo // 4 : hi // 4], src[:, lo // 4 : hi // 4]

        def quantize_y(c):
            h, inside = divmod(c * CH, HALF)
            nc.vector.quantize_mx(
                out=y_codes[h][:, inside : inside + CH].bitcast(FP8X4),
                scales=y_scales[:, c * CH : (c + 1) * CH],
                in_=yb[c][:].rearrange("p c t -> p (c t)"),
            )

        def store_words(h):
            nc.sync.dma_start(words_v[:, h * HALF : (h + 1) * HALF], y_codes[h][:].bitcast(I32))

        for j in (0, 1):
            project(j, 0, HALF, "bank%d" % j)
            store_rows(j, 1, 0)
        project(2, 0, HALF, "bank2", on_vector=True)
        store_rows(2, 1, 0)
        project(3, 0, CH, "bank3")
        project(3, CH, CH, "bank4", on_vector=True)
        store_rows(3, 1, 0)
        for c in (0, 1):
            nc.vector.tensor_copy(*weave_views(c, 0, CH))
        for c in (0, 1):
            quantize_y(c)
        for j in (0, 1):
            project(j, HALF, HALF, "bank%d" % (5 + j))
        store_rows(0, 2, 1)
        project(2, HALF, HALF, "bank7")
        project(3, HALF, CH, "bank0")
        project(3, HALF + CH, CH, "bank1")
        store_words(0)
        store_rows(2, 2, 1)
        nc.vector.tensor_copy(*weave_views(2, 0, CH - SCALAR_WEAVE))
        nc.vector.tensor_copy(*weave_views(3, 0, CH))
        nc.scalar.activation(*weave_views(2, CH - SCALAR_WEAVE, CH), IDENT)
        for c in (2, 3):
            quantize_y(c)
        store_words(1)
        for q in range(4):
            queue = nc.scalar if q < 2 else nc.sync
            queue.dma_start(scales_v[4 * q : 4 * q + 4, :], y_scales[32 * q : 32 * q + 4, :].bitcast(I32))
